import numpy as np, ml_dtypes
CORES = [10,34,74,98]
N = 4
import mx_ref
BF = ml_dtypes.bfloat16
def gcols(t, e):
    v = np.concatenate([t.reshape(8, 16, -1, 4), np.zeros((8, 16, 1, 4), BF)], axis=2)
    return np.ascontiguousarray(np.stack([v[g][:, e[g]] for g in range(8)])).reshape(128, -1)
def tile(rs):
    return np.stack(rs, axis=2).reshape(128, -1).astype(BF)
def pick(q, e):
    c = np.concatenate([q[0].reshape(128, -1, 4), np.zeros((128, 1, 4), np.uint8)], axis=1); s = np.concatenate([q[1], np.ones((16, 1), np.uint8)], axis=1)
    return (np.ascontiguousarray(c[:, e].reshape(128, -1)), np.ascontiguousarray(s[:, e]))
def join(*qs):
    return (np.concatenate([q[0] for q in qs], axis=1), np.concatenate([q[1] for q in qs], axis=1))
def put(q, e, v):
    c, s = q[0].reshape(128, -1, 4).copy(), q[1].copy(); c[:, e] = v[0].reshape(128, -1, 4); s[:, e] = v[1]
    return (c.reshape(128, -1), s)
def pk(c, s):
    return (np.ascontiguousarray(c), mx_ref.live(s))
def emit(q):
    return q[0], q[1]
def packed(v, rng):
    q = [mx_ref.quantize(np.ascontiguousarray(v[r])) for r in range(N)]
    return np.stack([a for a, b in q]), np.stack([mx_ref.plane(b, rng) for a, b in q])
def values_of_codes():
    e, c = np.zeros((128, 128, 4), np.float32), np.zeros((128, 2, 4), np.uint8)
    e[np.arange(128), np.arange(128), 0] = 1
    c[:127, :, 0] = np.arange(256).reshape(2, 128).T[:127]
    return mx_ref.matmul(mx_ref.quantize(e.reshape(128, 512).astype(BF)), (c.reshape(128, 8), np.full((16, 2), 127, np.uint8))).T.reshape(-1).astype(np.float64)
CODE_VALUE, SCALE_VALUE = values_of_codes(), 2.0 ** (np.arange(256) - 127.0)
def decode(q):
    return (CODE_VALUE[q[0]].reshape(16, 8, -1, 4) * SCALE_VALUE[q[1]][:, None, :, None] + 0.0).reshape(128, -1).astype(np.float32)
def f(rng, *shape):
    return mx_ref.flush((rng.standard_normal(shape, dtype=np.float32) * np.exp2(rng.integers(-2, 3, shape[:-1] + (1,)))).astype(BF))
def wide(rng, *shape, cols=0):
    v = rng.standard_normal(shape, dtype=np.float32) * np.exp2(rng.integers(-12, 13, shape)).astype(np.float32)
    if cols: v *= np.repeat(np.exp2(rng.integers(-cols, cols + 1, shape[:-2] + (1, shape[-1] // 4))) * (rng.random(shape[:-2] + (1, shape[-1] // 4)) > 0.0625), 4, axis=-1).astype(np.float32)
    return mx_ref.flush(v.astype(BF))
C, R = 448, 2
STEP = [2, 1]
def maxima(p):
    h = p[::16]
    m = np.zeros((8, C), bool)
    m[:, 1:-1] = (h[:, 1:-1] > h[:, :-2]) & (h[:, 1:-1] >= h[:, 2:])
    return m
def brackets(m):
    j = np.arange(C)
    a = np.maximum.accumulate(np.where(m, j, -1), axis=1)
    b = np.full((8, C), C - 1)
    b[:, :-1] = np.minimum.accumulate(np.where(m, j, C - 1)[:, ::-1], axis=1)[:, ::-1][:, 1:]
    return a, b, np.where(a[:, -1:] < 0, C - 1, a[:, -1:])
def half(s, t):
    return ((s.astype(np.float32) + t.astype(np.float32)) * np.float32(0.5)).astype(BF)
def numbers_of(rng):
    return {"x": np.array(f(rng, N, 128, 4 * C)), "u": np.array(f(rng, N, 128, 512)), "v": np.array(f(rng, N, 128, 512))}
def weights(rng, still=[]):
    w = np.array(f(rng, N, 128, 2048)).reshape(N, 8, 16, 4, 8, 16, 4)
    for i in still:
        w[:, :, i] = 0
        w[:, :, :, :, :, i] = 0
    c, p = packed(w.reshape(N, 128, 2048), rng)
    return {"wc": c, "ws": p}
def signs(rng):
    return np.stack([rng.permutation(8) % 2 * 2.0 - 1.0 for r in range(N)])
def setup_inputs(rng):
    return {**numbers_of(rng), **weights(rng)}
def setup_inputs_ties(rng):
    d = numbers_of(rng)
    e = rng.permutation(N)
    x = d["x"].reshape(N, 8, 16, C, 4)
    for r in range(N):
        k = np.zeros(C, int) if r == e[0] else rng.permutation(C) % 3
        a = x[r][:, :8, :3].copy()
        a[:, :, 2] = 0
        x[r][:, :8] = a[:, :, k]
    x[e[1]] = 0
    u = d["u"].reshape(N, 8, 16, 8, 16, 4)
    k = u.copy()
    u[:, :, :, :, 0] = 0
    for g in range(8): u[:, g, :8, g, 0] = k[:, g, :8, g, 0]
    return {"x": x.reshape(N, 128, 4 * C), "u": u.reshape(N, 128, 512), "v": d["v"], **weights(rng, range(8))}
def setup_inputs_near(rng):
    d = numbers_of(rng)
    x = d["x"].astype(np.float32).reshape(N, 8, 16, C, 4)
    u = d["u"].reshape(N, 128, 128, 4)
    u[:, :, ::16] = 0
    x[:, :, 0] = 0
    x[:, :, 8] = 0
    o, c = rng.permutation(N) % 4, signs(rng)
    for r in range(N):
        q = 2.0 ** -23 if o[r] < 2 else 2.0 ** -26
        if o[r] < 2: x[r, :, 0, :, 0] = c[r][:, None]
        s = rng.integers(0, 4, (8, C))
        s[:, :13] = [0, 2, 3, 3, 2, 2, 0, 1, 0, 1, 2, 0, 3]
        x[r, :, 8, :, 0] = s * q
        x[r, :, 9:] = rng.integers(4, 8, (8, 7, C, 4)) * q
        if o[r] == 3: x[r, :, 9, :, 0] = s * q
        k = 1.0 if o[r] % 2 == 0 else 2.0 ** -30
        for h in range(0, 128, 16):
            u[r, h, h, 0] = k
            u[r, h + 8, h, 0] = k
            if o[r] == 3:
                u[r, h + 8, h, 0] = 1.125 * k
                u[r, h + 9, h, 0] = -k
    return {"x": x.reshape(N, 128, 4 * C).astype(BF), "u": u.reshape(N, 128, 512), "v": d["v"], **weights(rng, [0, 8, 9, 10, 11, 12, 13, 14, 15])}
def setup_inputs_shapes(rng):
    d = numbers_of(rng)
    x = d["x"].astype(np.float32).reshape(N, 8, 16, C, 4)
    u = d["u"].reshape(N, 128, 128, 4)
    x[:, :, :11] = 0
    x[:, :, :8] = (9 + 4 * rng.integers(0, 2, (N, 8, 8, C, 4))) * np.exp2(-8.0 - np.arange(32).reshape(8, 1, 4) % 13)
    x[:, :, 0, :, 0] = 1.96875
    u[:, :, ::16] = 0
    j = np.arange(C)
    n = np.stack([rng.permutation(8) for r in range(N)])
    n[1] = n[0]
    size = np.where(rng.permutation(N) < N // 2, 2.0 ** -30, 1.0) * np.where(rng.permutation(N) < N // 2, -1.0, 1.0)
    for r in range(N):
        m = (1, C - 2)[r % 2]
        key = np.stack([0 * j + 5, j, C - 1 - np.abs(j - m), np.abs(j - m), j % 2, j // 2, (C - 1 - j) // 3, ((j == 1) | (j == C - 2)) + 0])[n[r]]
        z = ((key[:, :, None] >> np.arange(12)) & 1) * np.exp2(np.arange(12.0))
        for i in range(3): x[r, :, 8 + i] = z[:, :, 4 * i:4 * i + 4]
        for h in range(0, 128, 16): u[r, h + 8:h + 11, h] = size[r]
    return {"x": x.reshape(N, 128, 4 * C).astype(BF), "u": u.reshape(N, 128, 512), "v": d["v"], **weights(rng, range(11))}
def setup_inputs_huge(rng):
    d = numbers_of(rng)
    x = 0.55 + 0.35 * rng.random((N, 128, C, 4))
    a = 2.0 ** 30 * (1 - 0.1 * rng.random((N, 128, 8, 4))) * signs(rng)[:, None, :, None]
    h = np.where(np.arange(128) < 64, 1.0, -1.0)
    for r in rng.permutation(N)[:N // 2]:
        c = rng.permutation(C) % 2 * 2.0 - 1.0
        x[r] = 0.7 + 0.05 * rng.random((128, C, 4)) + 0.15 * h[:, None, None] * c[:, None]
        a[r] *= h[:, None, None]
    u = d["u"].reshape(N, 128, 128, 4)
    u[:, :, ::16] = a.astype(np.float32).astype(BF)
    w = np.zeros((N, 128, 4, 128, 4), np.float32)
    i = np.arange(128)
    for b in range(4): w[:, i, b, i, b] = 0.125
    wc, ws = packed(w.reshape(N, 128, 2048).astype(BF), rng)
    return {"x": (x * 2.0 ** 30).astype(np.float32).reshape(N, 128, 4 * C).astype(BF), "u": u.reshape(N, 128, 512), "v": d["v"], "wc": wc, "ws": ws}
def setup_inputs_spread(rng):
    d = setup_inputs(rng)
    d["x"] = wide(rng, N, 128, 4 * C, cols=6)
    return d
def check_inputs(d):
    b = []
    for k in ("x", "u", "v"):
        a = np.abs(d[k].astype(np.float32))
        if not (np.isfinite(a).all() and ((a == 0) | (a >= 2.0 ** -30) & (a <= 2.0 ** 30)).all()): b.append("a value of " + k)
    if ((d["wc"] & 0x7F) == 0x7F).any(): b.append("a code of wc that is no number")
    z = np.zeros((128, 4, 4), np.float32)
    z[:, 1] = 2.0 ** -30
    z[:, 2] = 2.0 ** 30
    c, s = emit(mx_ref.quantize(z.reshape(128, 16).astype(BF)))
    for r in range(N):
        p = mx_ref.live(d["ws"][r])
        if not ((p == s[0, 0]) | (p >= s[0, 1]) & (p <= s[0, 2])).all(): b.append("a scale of ws")
    return b
def reference(x, u, v, wc, ws):
    qu = [mx_ref.quantize(u[r]) for r in range(N)]
    lay = [pk(wc[r], ws[r]) for r in range(N)]
    now = [x[r] for r in range(N)]
    om = np.zeros((N, 8, C), np.float32)
    for t in range(R):
        full, ends, four, rest, sent = [], [], [], [], []
        for r in range(N):
            q = mx_ref.quantize(now[r])
            p = mx_ref.matmul(qu[r], q)
            hi, lo = maxima(p), maxima(-p)
            a, b, i = brackets(hi)
            c, d, k = brackets(lo)
            full.append(decode(q).astype(BF))
            ends.append(gcols(full[r], np.concatenate([i, k], axis=1)))
            four.append((np.where(a < 0, C, a), b, np.where(c < 0, C + 1, c), d))
            om[r] = 1.0 + hi - lo
        for r in range(N):
            z = np.concatenate([full[r], ends[(r - 1) % N]], axis=1)
            a, b, c, d = [gcols(z, k) for k in four[r]]
            e = half(half(a, b), half(c, d))
            rest.append((full[r].astype(np.float32) - e.astype(np.float32)).astype(BF))
            sent.append(mx_ref.quantize(e))
        now = [tile([mx_ref.matmul(pick(lay[r], np.arange(128 * b, 128 * b + 128)), sent[r ^ STEP[t]]) * np.float32(0.03125) + rest[r][:, b::4].astype(np.float32) for b in range(4)]) for r in range(N)]
    y = np.zeros((N, 128, C), np.float32)
    oc, osc = np.zeros((N, 128, 4 * C), np.uint8), np.zeros((N, 16, C), np.uint8)
    for r in range(N):
        q = mx_ref.quantize(now[r])
        y[r] = mx_ref.matmul(mx_ref.quantize(v[r]), q)
        oc[r], osc[r] = emit(q)
    return {"y": y, "om": om, "oc": oc, "osc": osc}

@@ -1,0 +1,406 @@
+from concourse.bass import DstId, RemoteDMATransfer
+from concourse.mybir import dt, AluOpType, ActivationFunctionType
+
+C = 448
+R = 2
+STEP = [2, 1]
+PAD = 16
+XO = 2 * PAD
+CH = [(0, 224), (224, 448)]
+SUB = [0, 112, 224, 336, 448]
+S1 = [0, 58, 112]
+LT = "float16"
+CODE = "float8_e4m3fn_x4"
+
+SCRATCH = {
+    "X0": ("sbuf", [128, XO + 4 * C], "bfloat16"),
+    "X1": ("sbuf", [128, XO + 4 * C], "bfloat16"),
+    "X2": ("sbuf", [128, XO + 4 * C], "bfloat16"),
+    "ub": ("sbuf", [128, 512], "bfloat16"),
+    "vb": ("sbuf", [128, 512], "bfloat16"),
+    "quc": ("sbuf", [128, 128], CODE), "qus": ("sbuf", [128, 128], "uint8"),
+    "qrc": ("sbuf", [128, 128], CODE), "qrs": ("sbuf", [128, 128], "uint8"),
+    "qvc": ("sbuf", [128, 128], CODE), "qvs": ("sbuf", [128, 128], "uint8"),
+    "wqc": ("sbuf", [128, 512], CODE), "wqs": ("sbuf", [128, 512], "uint8"),
+    "kc": ("sbuf", [128, 512], CODE), "ks": ("sbuf", [128, 512], "uint8"),
+    "kt": ("sbuf", [128, 516], "bfloat16"),
+    "pi": ("sbuf", [128, 2], "int32"),
+    "ci": ("sbuf", [128, 8], "int32"),
+    "cf": ("sbuf", [128, 8], "float32"),
+    "cd": ("sbuf", [128, 8], "float32"),
+    "dcol": ("sbuf", [128, 2], "float32"),
+    "uoi": ("sbuf", [128, 8], "int32"),
+    "uoff": ("sbuf", [128, 8], "uint16"),
+    "kf": ("sbuf", [128, 516], "float32"),
+    "hf": ("sbuf", [128, 450], "bfloat16"),
+    "r4": ("sbuf", [128, 452], "bfloat16"),
+    "V": ("sbuf", [128, 450], LT),
+    "S": ("sbuf", [128, 448], "bfloat16"),
+    "M4": ("sbuf", [128, 452], "bfloat16"),
+    "M2": ("sbuf", [128, 226], "bfloat16"),
+    "Pe": ("sbuf", [128, 224], "float32"),
+    "dd": ("sbuf", [128, 448], "bfloat16"),
+    "gg": ("sbuf", [128, 448], "bfloat16"),
+    "fl": ("sbuf", [128, 448], "bfloat16"),
+    "Ln": ("sbuf", [128, 448], LT),
+    "Rk": ("sbuf", [128, 448], LT),
+    "L2": ("sbuf", [128, 452], "bfloat16"),
+    "SA": ("sbuf", [128, 224], LT),
+    "SB": ("sbuf", [128, 224], LT),
+    "SV": ("sbuf", [128, 448], "bfloat16"),
+    "SS": ("sbuf", [128, 452], "bfloat16"),
+    "offE": ("sbuf", [128, 2], "uint16"),
+    "offA": ("sbuf", [128, 112], "uint16"),
+    "offB": ("sbuf", [128, 112], "uint16"),
+    "offV": ("sbuf", [128, 112], "uint16"),
+    "offS": ("sbuf", [128, 114], "uint16"),
+    "H": ("sbuf", [128, PAD + 4 * C], "bfloat16"),
+    "T1": ("sbuf", [128, 4 * C], "bfloat16"),
+    "AB": ("sbuf", [128, 4 * C], "bfloat16"),
+    "T2": ("sbuf", [128, 4 * C + 16], "bfloat16"),
+    "E": ("sbuf", [128, 4 * C], "bfloat16"),
+    "G": ("sbuf", [128, 4 * C], "bfloat16"),
+    "G32": ("sbuf", [128, 4 * C], "bfloat16"),
+    "X32": ("sbuf", [128, 4 * C], "bfloat16"),
+    "omA": ("sbuf", [128, C], "float32"),
+    "ysb": ("sbuf", [128, C], "float32"),
+    "PA": ("psum", [128, 2048], "float32"),
+    "PB": ("psum", [128, 2048], "float32"),
+}
+for _t in range(R + 1):
+    SCRATCH["qxc%d" % _t] = ("sbuf", [128, C + 16], CODE)
+    SCRATCH["qxs%d" % _t] = ("sbuf", [128, C + 16], "uint8")
+for _t in range(R):
+    SCRATCH["qnc%d" % _t] = ("sbuf", [128, 128], CODE)
+    SCRATCH["qns%d" % _t] = ("sbuf", [128, 128], "uint8")
+    SCRATCH["qec%d" % _t] = ("sbuf", [128, C], CODE)
+    SCRATCH["qes%d" % _t] = ("sbuf", [128, C], "uint8")
+    SCRATCH["lec%d" % _t] = ("sbuf", [128, C], CODE)
+    SCRATCH["les%d" % _t] = ("sbuf", [128, C], "uint8")
+
+SEMAPHORES = ["cv", "cs", "ct", "cg", "sent"]
+SEMAPHORES += ["d%d" % _i for _i in range(24)]
+SEMAPHORES += ["end%d" % _t for _t in range(R)]
+SEMAPHORES += ["arr%d_%d" % (_t, _k) for _t in range(R) for _k in range(len(CH))]
+
+A = AluOpType
+ACT = ActivationFunctionType
+U8 = dt.uint8
+U32 = dt.uint32
+
+
+def rank_program(g, core, T, topo):
+    rank = T.rank_of(core)
+    if rank is None:
+        return
+    N = len(T.cores)
+    Q = {"v": g.vector, "s": g.scalar, "t": g.tensor, "g": g, "y": g.sync}
+    CNT = {"v": "cv", "s": "cs", "t": "ct", "g": "cg"}
+    count = {"cv": 0, "cs": 0, "ct": 0, "cg": 0, "sent": 0}
+    waited = {e: {} for e in Q}
+    writer, readers = {}, {}
+    ndma = [0]
+
+    def wait(e, toks):
+        need = {}
+        for (sem, val, src) in toks:
+            if val > waited[e].get(sem, 0) and val > need.get(sem, 0):
+                need[sem] = val
+        for sem in need:
+            Q[e].wait_ge(T.sem[sem], need[sem])
+            waited[e][sem] = need[sem]
+
+    def deps(e, r, w):
+        toks = []
+        for k in r:
+            if k in writer:
+                toks.append(writer[k])
+            if k[:2] in ("PA", "PB"):
+                toks += [x for x in readers.get(k, []) if x[2] != e]
+        for k in w:
+            if k in writer:
+                toks.append(writer[k])
+            toks += readers.get(k, [])
+        return toks
+
+    def done(tok, r, w):
+        for k in r:
+            readers.setdefault(k, []).append(tok)
+        for k in w:
+            writer[k] = tok
+            readers[k] = []
+
+    def op(e, fn, r=(), w=(), extra=()):
+        wait(e, deps(e, r, w) + list(extra))
+        sem = CNT[e]
+        fn(Q[e]).then_inc(T.sem[sem], 1)
+        count[sem] += 1
+        done((sem, count[sem], e), r, w)
+
+    def dma(e, out, in_, r=(), w=(), extra=(), **kw):
+        wait(e, deps(e, r, w) + list(extra))
+        sem = "d%d" % ndma[0]
+        ndma[0] += 1
+        Q[e].dma_start(out, in_, **kw).then_inc(T.sem[sem], 16)
+        count[sem] = 16
+        tok = (sem, 16, "dma")
+        done(tok, r, w)
+        return tok
+
+    def maskof(es):
+        m = 0
+        for x in es:
+            m |= 1 << x
+        return m
+
+    right = T.cores[(rank + 1) % N]
+    left = T.cores[(rank - 1) % N]
+    X = [T.X0, T.X1, T.X2]
+    nch = len(CH)
+
+    tx = dma("y", T.X0[:, XO:XO + 4 * C], T.x[:], w=["X0_%d" % k for k in range(nch)])
+    dma("s", T.ub[:], T.u[:], w=["ub"])
+    dma("y", T.wqc[:].bitcast(U8), T.wc[:], w=["wqc"], extra=[tx])
+    dma("y", T.wqs[:], T.ws[:], w=["wqs"])
+    dma("y", T.vb[:], T.v[:], w=["vb"])
+
+    fi = dict(allow_small_or_imprecise_dtypes=True)
+    op("g", lambda q: q.iota(T.kf[:], [[1, 516]], 0, -4, **fi), w=["kf"])
+    op("g", lambda q: q.iota(T.pi[:, 0:1], [[0, 1]], 0, 1), w=["pi"])
+    op("g", lambda q: q.iota(T.uoi[:], [[16, 8]], 0, 0), w=["uoi"])
+    op("g", lambda q: q.iota(T.dcol[:, 0:1], [[0, 1]], 0, 4, **fi), w=["dcol"])
+    op("g", lambda q: q.iota(T.r4[:], [[0, 113], [1, 4]], 0, 0, **fi), w=["r4"])
+    op("g", lambda q: q.iota(T.hf[:], [[1, 225], [0, 2]], 0, 0, **fi), w=["hf"])
+
+    op("v", lambda q: q.memset(T.fl[:, 0:C:C - 1], 0.0), w=["fl"])
+    op("v", lambda q: q.memset(T.H[:, 0:PAD], 0.0), w=["Hp"])
+    op("v", lambda q: q.memset(T.L2[:, 0:1], 0.0), w=["L2a"])
+    op("v", lambda q: q.memset(T.L2[:, 449:452], 223.0 / 512), w=["L2b"])
+    op("v", lambda q: q.tensor_scalar(T.kt[:], T.kf[:], 3.0, None, A.is_equal), r=["kf"], w=["kt"])
+    for j, (sh, m) in enumerate([(0, 3), (2, 3), (2, 1), (2, 2), (0, 7)]):
+        op("v", lambda q: q.tensor_scalar(T.ci[:, j:j + 1], T.pi[:, 0:1], sh, m, A.logical_shift_right, A.bitwise_and),
+           r=["pi"], w=["ci%d" % j])
+    op("v", lambda q: q.tensor_copy(T.uoff[:], T.uoi[:]), r=["uoi"], w=["uoff"])
+    op("v", lambda q: q.tensor_copy(T.cf[:, 0:5], T.ci[:, 0:5]), r=["ci%d" % j for j in range(5)], w=["cf"])
+    ct, cq, cs, ch2, c8 = [T.cf[:, j:j + 1] for j in range(5)]
+    sgn, cA, cB, oms = [T.cd[:, j:j + 1] for j in range(4)]
+    op("s", lambda q: q.activation(sgn, cs, ACT.Identity, bias=1.0, scale=-2.0), r=["cf"], w=["sgn"])
+    op("s", lambda q: q.activation(cA, ct, ACT.Identity, bias=float(PAD - 4)), r=["cf"], w=["cA"])
+    op("s", lambda q: q.activation(cB, ct, ACT.Identity, bias=float(PAD + 4 * (C - 1))), r=["cf"], w=["cB"])
+    op("s", lambda q: q.activation(oms, cs, ACT.Identity, bias=1.0, scale=-1.0), r=["cf"], w=["oms"])
+    for b in range(4):
+        op("v", lambda q: q.quantize_mx(T.kc[:, 128 * b:128 * b + 128], T.ks[:, 128 * b:128 * b + 128],
+                                        T.kt[:, 3 - b:515 - b]), r=["kt"], w=["k%d" % b])
+    op("v", lambda q: q.quantize_mx(T.quc[:], T.qus[:], T.ub[:]), r=["ub"], w=["qu"])
+    op("v", lambda q: q.tensor_copy(T.qrc[:].bitcast(U32), T.quc[:].bitcast(U32).indirect(T.uoff[:])),
+       r=["qu", "uoff"], w=["qrc"])
+    op("s", lambda q: q.activation(T.qrs[:], T.qus[:].indirect(T.uoff[:]), ACT.Copy), r=["qu", "uoff"], w=["qrs"])
+    op("v", lambda q: q.tensor_scalar(T.V[:], T.kf[:, 0:450], T.dcol[:, 0:1], 1.0 / 512, A.add, A.mult),
+       r=["kf", "dcol"], w=["V"])
+
+    def xk(t):
+        if t == 0:
+            return ["X0_%d" % k for k in range(nch)]
+        return ["X%d_%d_%d" % (t, k, b) for k in range(nch) for b in range(4)]
+
+    def qk(t):
+        return ["qx%d_%d" % (t, k) for k in range(nch)]
+
+    op("v", lambda q: q.quantize_mx(T.qxc0[:, 0:C], T.qxs0[:, 0:C], T.X0[:, XO:XO + 4 * C]), r=xk(0), w=qk(0))
+    op("v", lambda q: q.tensor_scalar(T.M2[:, 0:225], T.r4[:, 0:450:2], ch2, None, A.is_equal), r=["r4", "cf"], w=["M2"])
+    op("v", lambda q: q.tensor_scalar(T.M4[:], T.r4[:], cq, None, A.is_equal), r=["r4", "cf"], w=["M4"])
+
+    def bank(P, b, a, z):
+        return P[:, 512 * b + a:512 * b + z]
+
+    def kq(b):
+        return T.kc[:, 128 * b:128 * b + 128], T.ks[:, 128 * b:128 * b + 128]
+
+    for t in range(R):
+        last = t == R - 1
+        partner = T.cores[rank ^ STEP[t]]
+        Xt, Xn = X[t], X[t + 1]
+        qc, qs = T["qxc%d" % t], T["qxs%d" % t]
+        qcn, qsn = T["qxc%d" % (t + 1)], T["qxs%d" % (t + 1)]
+        qnc, qns = T["qnc%d" % t], T["qns%d" % t]
+        qec, qes, lec, les = T["qec%d" % t], T["qes%d" % t], T["lec%d" % t], T["les%d" % t]
+
+        op("t", lambda q: q.matmul_mx(bank(T.PA, 0, 0, C), T.qrc[:], T.qrs[:], qc[:, 0:C], qs[:, 0:C], True, True),
+           r=qk(t) + ["qrc", "qrs"], w=["PA0"])
+        for b in range(4):
+            op("t", lambda q: q.matmul_mx(bank(T.PB, b, 0, C), kq(b)[0], kq(b)[1], qc[:, 0:C], qs[:, 0:C], True, True),
+               r=qk(t) + ["k%d" % b], w=["PB%d" % b])
+        op("s", lambda q: q.activation(Xt[:, PAD:XO], Xt[:, XO + 4 * C - PAD:XO + 4 * C], ACT.Copy),
+           r=xk(t), w=["X%dp" % t])
+        for b in range(4):
+            op("s", lambda q: q.activation(T.H[:, PAD + b:PAD + 4 * C:4], bank(T.PB, b, 0, C), ACT.Copy, scale=0.25),
+               r=["PB%d" % b], w=["H%d" % b])
+            if t == 0 and b == 2:
+                op("s", lambda q: q.activation(T.S[:], T.hf[:, 1:449], ACT.Copy, scale=1.0 / 512), r=["hf"], w=["S"])
+
+        op("v", lambda q: q.tensor_copy(T.Pe[:], T.PA[:, 0:C:2]), r=["PA0"], w=["Pe"])
+        op("v", lambda q: q.tensor_tensor(T.dd[:, 1:C:2], T.PA[:, 1:C:2], T.Pe[:], A.subtract), r=["PA0", "Pe"], w=["d1"])
+        op("v", lambda q: q.tensor_tensor(T.dd[:, 2:C:2], T.Pe[:, 1:224], T.PA[:, 1:C - 2:2], A.subtract),
+           r=["PA0", "Pe"], w=["d0"])
+        op("v", lambda q: q.tensor_scalar(T.gg[:, 1:C], T.dd[:, 1:C], sgn, 0.0, A.mult, A.is_gt),
+           r=["d0", "d1", "sgn"], w=["gg"])
+        op("v", lambda q: q.tensor_tensor(T.fl[:, 1:C - 1], T.gg[:, 1:C - 1], T.gg[:, 2:C], A.is_gt), r=["gg"], w=["fl"])
+        op("v", lambda q: q.tensor_tensor_scan(T.Ln[:], T.fl[:], T.V[:, 1:C + 1], 0.0, A.max, A.min),
+           r=["fl", "V"], w=["Ln"])
+        op("v", lambda q: q.tensor_scalar(T.offE[:, 0:1], T.Ln[:, C - 1:C], 2048.0, cA, A.mult, A.add),
+           r=["Ln", "cA"], w=["offE"])
+        op("v", lambda q: q.tensor_copy(Xt[:, 0:PAD], Xt[:, PAD:XO + 4 * C].indirect(T.offE[:, 0:1])),
+           r=xk(t) + ["X%dp" % t, "offE"], w=["ET%d" % t])
+        op("v", lambda q: q.quantize_mx(qnc[:], qns[:], Xt[:, 0:512]), r=["ET%d" % t], w=["qn%d" % t])
+        wait("g", deps("g", ["qn%d" % t], []))
+        es = topo.engines(core, right)
+        rid, pid = topo.addr(right)[:2]
+        g.remote_dma_fused([
+            RemoteDMATransfer(dst_ids=[DstId(rid=rid, pnc=pid)], dma_engine_mask=maskof(es[0::2]),
+                              remote_sem=T.sem["end%d" % t], src=qnc[:, 0:2].bitcast(U8), dst=qc[:, C:C + 2].bitcast(U8)),
+            RemoteDMATransfer(dst_ids=[DstId(rid=rid, pnc=pid)], dma_engine_mask=maskof(es[1::2]),
+                              remote_sem=T.sem["end%d" % t], src=qns[:, 0:8], dst=qs[:, C:C + 8]),
+        ], local_sem=T.sem.sent)
+        count["sent"] += len(es)
+        nend = len(topo.engines(left, core))
+        count["end%d" % t] = nend
+
+        op("v", lambda q: q.tensor_tensor_scan(T.SA[:], T.M2[:, 0:224], T.Ln[:, 0:C:2], 0.0, A.max, A.min),
+           r=["Ln", "M2"], w=["SA"])
+        op("v", lambda q: q.tensor_tensor_scan(T.Rk[:, 0:C - 1], T.fl[:, C - 1:0:-1], T.V[:, 0:C - 1], 0.0, A.max, A.min),
+           r=["fl", "V"], w=["Rk"])
+        op("v", lambda q: q.tensor_scalar(T.offA[:], T.SA[:, 1:224:2], 2048.0, cA, A.mult, A.add),
+           r=["SA", "cA"], w=["offA"])
+
+        hk = ["H%d" % b for b in range(4)] + ["Hp"]
+        for k in range(len(S1) - 1):
+            a, z = S1[k], S1[k + 1]
+            op("s", lambda q: q.activation(T.T1[:, 16 * a:16 * z], T.H[:].indirect(T.offA[:, a:z]), ACT.Copy),
+               r=hk + ["offA"], w=["T1_%d" % k])
+
+        op("v", lambda q: q.tensor_tensor_scan(T.SB[:], T.M2[:, 1:225], T.Rk[:, 0:C - 1:2], 0.0, A.max, A.min),
+           r=["Rk", "M2"], w=["SB"])
+        op("v", lambda q: q.tensor_tensor_scan(T.L2[:, 1:C + 1], T.fl[:], T.S[:], 0.0, A.max, A.min),
+           r=["fl", "S"], w=["L2"])
+        op("v", lambda q: q.tensor_scalar(T.offB[:], T.SB[:, 223:0:-2], -2048.0, cB, A.mult, A.add),
+           r=["SB", "cB"], w=["offB"])
+        op("v", lambda q: q.tensor_tensor_scan(T.SS[:], T.M4[:], T.L2[:], 0.0, A.max, A.min),
+           r=["L2", "L2a", "L2b", "M4"], w=["SS"])
+        op("v", lambda q: q.tensor_tensor_scan(T.SV[:], T.M4[:, 0:C], T.L2[:, 1:C + 1], 0.0, A.max, A.min),
+           r=["L2", "M4"], w=["SV"])
+        op("v", lambda q: q.tensor_scalar(T.offS[:, 0:113], T.SS[:, 3:452:4], 4096.0, c8, A.mult, A.add),
+           r=["SS", "cf"], w=["offS"])
+        op("v", lambda q: q.tensor_scalar(T.offV[:], T.SV[:, 3:C:4], 4096.0, c8, A.mult, A.add),
+           r=["SV", "cf"], w=["offV"])
+
+        fx = ["ABf%d" % e for e in range(8)]
+        for k in range(len(S1) - 1):
+            a, z = S1[k], S1[k + 1]
+            op("v", lambda q: q.tensor_tensor(T.AB[:, 16 * a:16 * z], T.H[:].indirect(T.offB[:, a:z]),
+                                              T.T1[:, 16 * a:16 * z], A.add),
+               r=hk + ["offB", "T1_%d" % k], w=["AB%d" % k] + (fx if k == 0 else []))
+
+        if last:
+            op("s", lambda q: q.activation(T.omA[:], T.fl[:], ACT.Identity, bias=oms, scale=sgn),
+               r=["fl", "oms", "sgn"], w=["omA"])
+            dma("y", T.om[:], T.omA[0:128:16, :], r=["omA"], w=["om"])
+
+        for b in range(4):
+            op("t", lambda q: q.matmul_mx(bank(T.PA, b, 0, 128), kq(b)[0], kq(b)[1], qc[:, C - 126:C + 2],
+                                          qs[:, C - 126:C + 2], True, True),
+               r=qk(t) + ["k%d" % b], w=["PA%d" % b], extra=[("end%d" % t, nend, "r")])
+        for b in range(4):
+            for s in range(2):
+                e = 4 * s + b
+                op("s", lambda q: q.activation(T.AB[:, e:e + 1], bank(T.PA, b, 126 + s, 127 + s), ACT.Identity,
+                                               bias=T.AB[:, e:e + 1], scale=0.25),
+                   r=["PA%d" % b, "AB0"], w=["ABf%d" % e])
+
+        ns = len(SUB) - 1
+        sb = [0] + [SUB[k] // 4 + 2 for k in range(1, ns)] + [113]
+
+        def win(n1):
+            upto = 1
+            while 2 * S1[upto] - 1 < min((n1 + 1) // 2, 223):
+                upto += 1
+            return T.AB[:, 0:16 * S1[upto]], ["AB%d" % k for k in range(upto)] + fx
+
+        for k in range(ns):
+            a, z = sb[k], sb[k + 1]
+            wv, keys = win(4 * z - 2)
+            op("s", lambda q: q.activation(T.T2[:, 16 * a:16 * z], wv.indirect(T.offS[:, a:z]), ACT.Copy),
+               r=keys + ["offS"], w=["T2_%d" % k])
+        es = topo.engines(core, partner)
+        rid, pid = topo.addr(partner)[:2]
+        narr = 2 * len(topo.engines(partner, core))
+        for k in range(ns):
+            a, z = SUB[k], SUB[k + 1]
+            wv, keys = win(z - 1)
+            op("v", lambda q: q.tensor_tensor(T.E[:, 4 * a:4 * z], wv.indirect(T.offV[:, a // 4:z // 4]),
+                                              T.T2[:, 4 * a + 4:4 * z + 4], A.add),
+               r=keys + ["offV"] + ["T2_%d" % j for j in range(k + 1)], w=["E%d" % k])
+            for j, (c0, c1) in enumerate(CH):
+                if c1 != z:
+                    continue
+                op("v", lambda q: q.quantize_mx(qec[:, c0:c1], qes[:, c0:c1], T.E[:, 4 * c0:4 * c1]),
+                   r=["E%d" % i for i in range(k + 1)], w=["qe%d_%d" % (t, j)])
+                wait("g", deps("g", ["qe%d_%d" % (t, j)], []))
+                sem = "arr%d_%d" % (t, j)
+                g.remote_dma(lec[:, c0:c1].bitcast(U8), qec[:, c0:c1].bitcast(U8), T.sem[sem], T.sem.sent, pid, rid,
+                             maskof(es))
+                g.remote_dma(les[:, c0:c1], qes[:, c0:c1], T.sem[sem], T.sem.sent, pid, rid, maskof(es))
+                count["sent"] += 2 * len(es)
+                count[sem] = narr
+
+        ek = ["E%d" % i for i in range(ns)]
+        for b in range(4):
+            op("v", lambda q: q.tensor_tensor(T.G[:, C * b:C * b + C], bank(T.PB, b, 0, C), T.E[:, b:4 * C:4], A.subtract),
+               r=ek + ["PB%d" % b], w=["G%d" % b])
+            op("s", lambda q: q.activation(T.G32[:, C * b:C * b + C], T.G[:, C * b:C * b + C], ACT.Copy, scale=32.0),
+               r=["G%d" % b], w=["G32_%d" % b])
+        if t == 0:
+            op("v", lambda q: q.quantize_mx(T.qvc[:], T.qvs[:], T.vb[:]), r=["vb"], w=["qv"])
+        if last:
+            dma("g", T.om[:], T.omA[4:128:16, :], r=["omA"], w=["om"], accum_op=A.add)
+
+        for j, (c0, c1) in enumerate(CH):
+            P, pn = (T.PA, "PA") if j % 2 == 0 else (T.PB, "PB")
+            n = c1 - c0
+            for b in range(4):
+                op("t", lambda q: q.matmul_mx(bank(P, b, 0, n), T.wqc[:, 128 * b:128 * b + 128],
+                                              T.wqs[:, 128 * b:128 * b + 128], lec[:, c0:c1], les[:, c0:c1], True, True),
+                   r=["wqc", "wqs"], w=["%s%d" % (pn, b)], extra=[("arr%d_%d" % (t, j), narr, "r")])
+            for b in range(4):
+                o = C * b
+                op("v", lambda q: q.tensor_tensor(T.X32[:, o + c0:o + c1], bank(P, b, 0, n), T.G32[:, o + c0:o + c1], A.add),
+                   r=["%s%d" % (pn, b), "G32_%d" % b], w=["X32_%d_%d" % (j, b)])
+                dst = Xn[:, XO + 4 * c0 + b:XO + 4 * c1:4]
+                kw = dict(r=["X32_%d_%d" % (j, b)], w=["X%d_%d_%d" % (t + 1, j, b)])
+                if b < 3:
+                    op("s", lambda q: q.activation(dst, T.X32[:, o + c0:o + c1], ACT.Copy, scale=0.03125), **kw)
+                else:
+                    op("v", lambda q: q.tensor_scalar(dst, T.X32[:, o + c0:o + c1], 0.03125, None, A.mult), **kw)
+            op("v", lambda q: q.quantize_mx(qcn[:, c0:c1], qsn[:, c0:c1], Xn[:, XO + 4 * c0:XO + 4 * c1]),
+               r=["X%d_%d_%d" % (t + 1, j, b) for b in range(4)], w=["qx%d_%d" % (t + 1, j)])
+            if last and j < nch - 1:
+                dma("y", T.oc[:, 4 * c0:4 * c1], qcn[:, c0:c1].bitcast(U8), r=["qx%d_%d" % (t + 1, j)])
+
+    qcn, qsn = T["qxc%d" % R], T["qxs%d" % R]
+    for j, (c0, c1) in enumerate(CH):
+        n = c1 - c0
+        key = "qx%d_%d" % (R, j)
+        fin = j == nch - 1
+        yb = "PA%d" % j
+        op("t", lambda q: q.matmul_mx(bank(T.PA, j, 0, n), T.qvc[:], T.qvs[:], qcn[:, c0:c1], qsn[:, c0:c1], True, True),
+           r=[key, "qv"], w=[yb])
+        if not fin:
+            op("s", lambda q: q.activation(T.ysb[:, c0:c1], bank(T.PA, j, 0, n), ACT.Copy), r=[yb], w=["ysb%d" % j])
+            dma("y", T.y[:, c0:c1], T.ysb[:, c0:c1], r=["ysb%d" % j])
+        else:
+            dma("y", T.oc[:, 4 * c0:4 * c1], qcn[:, c0:c1].bitcast(U8), r=[key])
+            for k in range(4):
+                dma("s" if k < 2 else "y", T.osc[4 * k:4 * k + 4, :], qsn[32 * k:32 * k + 4, 0:C], r=qk(R))
+            op("v", lambda q: q.tensor_copy(T.ysb[:, c0:c1], bank(T.PA, j, 0, n)), r=[yb], w=["ysb%d" % j])
+            dma("s", T.y[:, c0:c1], T.ysb[:, c0:c1], r=["ysb%d" % j])
+
+    wait("g", [(sem, count[sem], "x") for sem in count if count[sem] > 0])

@@ -7,76 +7,27 @@ STEP = [2, 1]
 PAD = 16
 XO = 2 * PAD
 CH = [(0, 224), (224, 448)]
-SUB = [0, 112, 224, 336, 448]
+SUB = [0, 112, 224, 248, 344, 448]
 S1 = [0, 58, 112]
-LT = "float16"
 CODE = "float8_e4m3fn_x4"
 
-SCRATCH = {
-    "X0": ("sbuf", [128, XO + 4 * C], "bfloat16"),
-    "X1": ("sbuf", [128, XO + 4 * C], "bfloat16"),
-    "X2": ("sbuf", [128, XO + 4 * C], "bfloat16"),
-    "ub": ("sbuf", [128, 512], "bfloat16"),
-    "vb": ("sbuf", [128, 512], "bfloat16"),
-    "quc": ("sbuf", [128, 128], CODE), "qus": ("sbuf", [128, 128], "uint8"),
-    "qrc": ("sbuf", [128, 128], CODE), "qrs": ("sbuf", [128, 128], "uint8"),
-    "qvc": ("sbuf", [128, 128], CODE), "qvs": ("sbuf", [128, 128], "uint8"),
-    "wqc": ("sbuf", [128, 512], CODE), "wqs": ("sbuf", [128, 512], "uint8"),
-    "kc": ("sbuf", [128, 512], CODE), "ks": ("sbuf", [128, 512], "uint8"),
-    "kt": ("sbuf", [128, 516], "bfloat16"),
-    "pi": ("sbuf", [128, 2], "int32"),
-    "ci": ("sbuf", [128, 8], "int32"),
-    "cf": ("sbuf", [128, 8], "float32"),
-    "cd": ("sbuf", [128, 8], "float32"),
-    "dcol": ("sbuf", [128, 2], "float32"),
-    "uoi": ("sbuf", [128, 8], "int32"),
-    "uoff": ("sbuf", [128, 8], "uint16"),
-    "kf": ("sbuf", [128, 516], "float32"),
-    "hf": ("sbuf", [128, 450], "bfloat16"),
-    "r4": ("sbuf", [128, 452], "bfloat16"),
-    "V": ("sbuf", [128, 450], LT),
-    "S": ("sbuf", [128, 448], "bfloat16"),
-    "M4": ("sbuf", [128, 452], "bfloat16"),
-    "M2": ("sbuf", [128, 226], "bfloat16"),
-    "Pe": ("sbuf", [128, 224], "float32"),
-    "dd": ("sbuf", [128, 448], "bfloat16"),
-    "gg": ("sbuf", [128, 448], "bfloat16"),
-    "fl": ("sbuf", [128, 448], "bfloat16"),
-    "Ln": ("sbuf", [128, 448], LT),
-    "Rk": ("sbuf", [128, 448], LT),
-    "L2": ("sbuf", [128, 452], "bfloat16"),
-    "SA": ("sbuf", [128, 224], LT),
-    "SB": ("sbuf", [128, 224], LT),
-    "SV": ("sbuf", [128, 448], "bfloat16"),
-    "SS": ("sbuf", [128, 452], "bfloat16"),
-    "offE": ("sbuf", [128, 2], "uint16"),
-    "offA": ("sbuf", [128, 112], "uint16"),
-    "offB": ("sbuf", [128, 112], "uint16"),
-    "offV": ("sbuf", [128, 112], "uint16"),
-    "offS": ("sbuf", [128, 114], "uint16"),
-    "H": ("sbuf", [128, PAD + 4 * C], "bfloat16"),
-    "T1": ("sbuf", [128, 4 * C], "bfloat16"),
-    "AB": ("sbuf", [128, 4 * C], "bfloat16"),
-    "T2": ("sbuf", [128, 4 * C + 16], "bfloat16"),
-    "E": ("sbuf", [128, 4 * C], "bfloat16"),
-    "G": ("sbuf", [128, 4 * C], "bfloat16"),
-    "G32": ("sbuf", [128, 4 * C], "bfloat16"),
-    "X32": ("sbuf", [128, 4 * C], "bfloat16"),
-    "omA": ("sbuf", [128, C], "float32"),
-    "ysb": ("sbuf", [128, C], "float32"),
-    "PA": ("psum", [128, 2048], "float32"),
-    "PB": ("psum", [128, 2048], "float32"),
-}
-for _t in range(R + 1):
-    SCRATCH["qxc%d" % _t] = ("sbuf", [128, C + 16], CODE)
-    SCRATCH["qxs%d" % _t] = ("sbuf", [128, C + 16], "uint8")
-for _t in range(R):
-    SCRATCH["qnc%d" % _t] = ("sbuf", [128, 128], CODE)
-    SCRATCH["qns%d" % _t] = ("sbuf", [128, 128], "uint8")
-    SCRATCH["qec%d" % _t] = ("sbuf", [128, C], CODE)
-    SCRATCH["qes%d" % _t] = ("sbuf", [128, C], "uint8")
-    SCRATCH["lec%d" % _t] = ("sbuf", [128, C], CODE)
-    SCRATCH["les%d" % _t] = ("sbuf", [128, C], "uint8")
+SCRATCH = {"PA": ("psum", [128, 2048], "float32"), "PB": ("psum", [128, 2048], "float32")}
+for _d, _l in {
+    "bfloat16": [("X0", XO + 4 * C), ("X1", XO + 4 * C), ("X2", XO + 4 * C), ("ub", 512), ("vb", 512), ("kt", 516),
+                 ("kf", 516), ("hf", 226), ("r4", 452), ("S", C), ("M4", 452), ("M2", 226), ("dd", C), ("gg", C),
+                 ("fl", C), ("L2", 452), ("SV", C), ("SS", 452), ("H", PAD + 4 * C), ("T1", 4 * C), ("AB", 4 * C),
+                 ("T2", 4 * C + 16), ("E", 4 * C), ("G", 4 * C), ("G32", 4 * C), ("X32", 4 * C)],
+    "float16": [("V", 450), ("Ln", C), ("Rk", C), ("SA", 224), ("SB", 224)],
+    "float32": [("cf", 8), ("cd", 8), ("Pe", 224), ("omA", C), ("ysb", C)],
+    "int32": [("pi", 2), ("ci", 8), ("uoi", 8)],
+    "uint16": [("uoff", 8), ("offE", 2), ("offA", 112), ("offB", 112), ("offV", 112), ("offS", 114)],
+}.items():
+    for _n, _w in _l:
+        SCRATCH[_n] = ("sbuf", [128, _w], _d)
+for _n, _w in [("qu", 128), ("qr", 128), ("qv", 128), ("wq", 512), ("k", 512), ("x0", C + 16), ("x1", C + 16),
+               ("x2", C + 16), ("n0", 128), ("n1", 128), ("e0", C), ("e1", C), ("l0", C), ("l1", C)]:
+    SCRATCH[_n + "c"] = ("sbuf", [128, _w], CODE)
+    SCRATCH[_n + "s"] = ("sbuf", [128, _w], "uint8")
 
 SEMAPHORES = ["cv", "cs", "ct", "cg", "sent"]
 SEMAPHORES += ["d%d" % _i for _i in range(24)]
@@ -153,50 +104,78 @@ def rank_program(g, core, T, topo):
             m |= 1 << x
         return m
 
+    def ts(out, in0, s1, s2, o0, o1, r, w):
+        if s2 is None:
+            op("v", lambda q: q.tensor_scalar(out, in0, s1, None, o0), r, w)
+        else:
+            op("v", lambda q: q.tensor_scalar(out, in0, s1, s2, o0, o1), r, w)
+
+    def tt(out, in0, in1, o, r, w):
+        op("v", lambda q: q.tensor_tensor(out, in0, in1, o), r, w)
+
+    def cp(out, in_, r, w):
+        op("v", lambda q: q.tensor_copy(out, in_), r, w)
+
+    def hold(out, pick, val, r, w):
+        op("v", lambda q: q.tensor_tensor_scan(out, pick, val, 0.0, A.max, A.min), r, w)
+
+    def act(out, in_, r, w, func=ACT.Copy, **kw):
+        op("s", lambda q: q.activation(out, in_, func, **kw), r, w)
+
+    def quant(name, a, z, in_, r, w):
+        op("v", lambda q: q.quantize_mx(T[name + "c"][:, a:z], T[name + "s"][:, a:z], in_), r, w)
+
+    def bank(P, b, a, z, step=1):
+        return P[:, 512 * b + a:512 * b + z:step]
+
+    def mm(P, b, wn, wa, xn, a, z, r, extra=()):
+        op("t", lambda q: q.matmul_mx(T[P][:, 512 * b:512 * b + z - a], T[wn + "c"][:, wa:wa + 128],
+                                      T[wn + "s"][:, wa:wa + 128], T[xn + "c"][:, a:z], T[xn + "s"][:, a:z], True, True),
+           r, ["%s%d" % (P, b)], extra)
+
     right = T.cores[(rank + 1) % N]
     left = T.cores[(rank - 1) % N]
     X = [T.X0, T.X1, T.X2]
     nch = len(CH)
+    M = CH[0][1]
 
-    tx = dma("y", T.X0[:, XO:XO + 4 * C], T.x[:], w=["X0_%d" % k for k in range(nch)])
+    tx = dma("y", T.X0[:, XO:XO + 4 * C], T.x[:], w=["X0_0", "X0_1"])
     dma("s", T.ub[:], T.u[:], w=["ub"])
     dma("y", T.wqc[:].bitcast(U8), T.wc[:], w=["wqc"], extra=[tx])
     dma("y", T.wqs[:], T.ws[:], w=["wqs"])
     dma("y", T.vb[:], T.v[:], w=["vb"])
 
     fi = dict(allow_small_or_imprecise_dtypes=True)
-    op("g", lambda q: q.iota(T.kf[:], [[1, 516]], 0, -4, **fi), w=["kf"])
     op("g", lambda q: q.iota(T.pi[:, 0:1], [[0, 1]], 0, 1), w=["pi"])
     op("g", lambda q: q.iota(T.uoi[:], [[16, 8]], 0, 0), w=["uoi"])
-    op("g", lambda q: q.iota(T.dcol[:, 0:1], [[0, 1]], 0, 4, **fi), w=["dcol"])
+    op("g", lambda q: q.iota(T.kf[:], [[1, 516]], 0, -4, **fi), w=["kf"])
+    op("g", lambda q: q.iota(T.hf[:], [[1, 226]], 0, 0, **fi), w=["hf"])
     op("g", lambda q: q.iota(T.r4[:], [[0, 113], [1, 4]], 0, 0, **fi), w=["r4"])
-    op("g", lambda q: q.iota(T.hf[:], [[1, 225], [0, 2]], 0, 0, **fi), w=["hf"])
 
-    op("v", lambda q: q.memset(T.fl[:, 0:C:C - 1], 0.0), w=["fl"])
+    op("v", lambda q: q.memset(T.fl[:, 0:C:C - 1], 0.0), w=["flp"])
     op("v", lambda q: q.memset(T.H[:, 0:PAD], 0.0), w=["Hp"])
+    for j, (sh, m) in enumerate([(0, 3), (2, 3), (2, 1), (2, 2), (0, 7)]):
+        ts(T.ci[:, j:j + 1], T.pi[:, 0:1], sh, m, A.logical_shift_right, A.bitwise_and, ["pi"], ["ci%d" % j])
+    cp(T.uoff[:], T.uoi[:], ["uoi"], ["uoff"])
     op("v", lambda q: q.memset(T.L2[:, 0:1], 0.0), w=["L2a"])
     op("v", lambda q: q.memset(T.L2[:, 449:452], 223.0 / 512), w=["L2b"])
-    op("v", lambda q: q.tensor_scalar(T.kt[:], T.kf[:], 3.0, None, A.is_equal), r=["kf"], w=["kt"])
-    for j, (sh, m) in enumerate([(0, 3), (2, 3), (2, 1), (2, 2), (0, 7)]):
-        op("v", lambda q: q.tensor_scalar(T.ci[:, j:j + 1], T.pi[:, 0:1], sh, m, A.logical_shift_right, A.bitwise_and),
-           r=["pi"], w=["ci%d" % j])
-    op("v", lambda q: q.tensor_copy(T.uoff[:], T.uoi[:]), r=["uoi"], w=["uoff"])
-    op("v", lambda q: q.tensor_copy(T.cf[:, 0:5], T.ci[:, 0:5]), r=["ci%d" % j for j in range(5)], w=["cf"])
+    cp(T.cf[:, 0:5], T.ci[:, 0:5], ["ci%d" % j for j in range(5)], ["cf"])
     ct, cq, cs, ch2, c8 = [T.cf[:, j:j + 1] for j in range(5)]
     sgn, cA, cB, oms = [T.cd[:, j:j + 1] for j in range(4)]
-    op("s", lambda q: q.activation(sgn, cs, ACT.Identity, bias=1.0, scale=-2.0), r=["cf"], w=["sgn"])
-    op("s", lambda q: q.activation(cA, ct, ACT.Identity, bias=float(PAD - 4)), r=["cf"], w=["cA"])
-    op("s", lambda q: q.activation(cB, ct, ACT.Identity, bias=float(PAD + 4 * (C - 1))), r=["cf"], w=["cB"])
-    op("s", lambda q: q.activation(oms, cs, ACT.Identity, bias=1.0, scale=-1.0), r=["cf"], w=["oms"])
+    act(sgn, cs, ["cf"], ["sgn"], ACT.Identity, bias=1.0, scale=-2.0)
+    act(cA, ct, ["cf"], ["cA"], ACT.Identity, bias=float(PAD - 4))
+    act(cB, ct, ["cf"], ["cB"], ACT.Identity, bias=float(PAD + 4 * (C - 1)))
+    act(oms, cs, ["cf"], ["oms"], ACT.Identity, bias=1.0, scale=-1.0)
+    ts(T.kt[:], T.kf[:], 3.0, None, A.is_equal, None, ["kf"], ["kt"])
     for b in range(4):
-        op("v", lambda q: q.quantize_mx(T.kc[:, 128 * b:128 * b + 128], T.ks[:, 128 * b:128 * b + 128],
-                                        T.kt[:, 3 - b:515 - b]), r=["kt"], w=["k%d" % b])
-    op("v", lambda q: q.quantize_mx(T.quc[:], T.qus[:], T.ub[:]), r=["ub"], w=["qu"])
-    op("v", lambda q: q.tensor_copy(T.qrc[:].bitcast(U32), T.quc[:].bitcast(U32).indirect(T.uoff[:])),
-       r=["qu", "uoff"], w=["qrc"])
-    op("s", lambda q: q.activation(T.qrs[:], T.qus[:].indirect(T.uoff[:]), ACT.Copy), r=["qu", "uoff"], w=["qrs"])
-    op("v", lambda q: q.tensor_scalar(T.V[:], T.kf[:, 0:450], T.dcol[:, 0:1], 1.0 / 512, A.add, A.mult),
-       r=["kf", "dcol"], w=["V"])
+        quant("k", 128 * b, 128 * b + 128, T.kt[:, 3 - b:515 - b], ["kt"], ["k%d" % b])
+    quant("qu", 0, 128, T.ub[:], ["ub"], ["qu"])
+    ts(T.V[:, 0:450:2], T.hf[:, 0:225], 1.0 / 256, None, A.mult, None, ["hf"], ["V0"])
+    ts(T.V[:, 1:450:2], T.hf[:, 0:225], 1.0 / 256, 1.0 / 512, A.mult, A.add, ["hf"], ["V1"])
+    cp(T.qrc[:].bitcast(U32), T.quc[:].bitcast(U32).indirect(T.uoff[:]), ["qu", "uoff"], ["qrc"])
+    act(T.qrs[:], T.qus[:].indirect(T.uoff[:]), ["qu", "uoff"], ["qrs"])
+    act(T.S[:, 0:C:2], T.hf[:, 0:224], ["hf"], ["S0"], scale=1.0 / 512)
+    act(T.S[:, 1:C:2], T.hf[:, 1:225], ["hf"], ["S1"], scale=1.0 / 512)
 
     def xk(t):
         if t == 0:
@@ -206,118 +185,91 @@ def rank_program(g, core, T, topo):
     def qk(t):
         return ["qx%d_%d" % (t, k) for k in range(nch)]
 
-    op("v", lambda q: q.quantize_mx(T.qxc0[:, 0:C], T.qxs0[:, 0:C], T.X0[:, XO:XO + 4 * C]), r=xk(0), w=qk(0))
-    op("v", lambda q: q.tensor_scalar(T.M2[:, 0:225], T.r4[:, 0:450:2], ch2, None, A.is_equal), r=["r4", "cf"], w=["M2"])
-    op("v", lambda q: q.tensor_scalar(T.M4[:], T.r4[:], cq, None, A.is_equal), r=["r4", "cf"], w=["M4"])
-
-    def bank(P, b, a, z):
-        return P[:, 512 * b + a:512 * b + z]
-
-    def kq(b):
-        return T.kc[:, 128 * b:128 * b + 128], T.ks[:, 128 * b:128 * b + 128]
+    quant("x0", 0, M, T.X0[:, XO:XO + 4 * M], ["X0_0"], ["qx0_0"])
+    quant("x0", M, C, T.X0[:, XO + 4 * M:XO + 4 * C], ["X0_1"], ["qx0_1"])
+    ts(T.M2[:, 0:225], T.r4[:, 0:450:2], ch2, None, A.is_equal, None, ["r4", "cf"], ["M2"])
+    ts(T.M4[:], T.r4[:], cq, None, A.is_equal, None, ["r4", "cf"], ["M4"])
 
     for t in range(R):
         last = t == R - 1
         partner = T.cores[rank ^ STEP[t]]
         Xt, Xn = X[t], X[t + 1]
-        qc, qs = T["qxc%d" % t], T["qxs%d" % t]
-        qcn, qsn = T["qxc%d" % (t + 1)], T["qxs%d" % (t + 1)]
-        qnc, qns = T["qnc%d" % t], T["qns%d" % t]
-        qec, qes, lec, les = T["qec%d" % t], T["qes%d" % t], T["lec%d" % t], T["les%d" % t]
+        xn, nn, en, ln = "x%d" % t, "n%d" % t, "e%d" % t, "l%d" % t
 
-        op("t", lambda q: q.matmul_mx(bank(T.PA, 0, 0, C), T.qrc[:], T.qrs[:], qc[:, 0:C], qs[:, 0:C], True, True),
-           r=qk(t) + ["qrc", "qrs"], w=["PA0"])
+        mm("PA", 0, "qr", 0, xn, 0, M, ["qx%d_0" % t, "qrc", "qrs"])
+        mm("PA", 1, "qr", 0, xn, M - 2, C, qk(t) + ["qrc", "qrs"])
         for b in range(4):
-            op("t", lambda q: q.matmul_mx(bank(T.PB, b, 0, C), kq(b)[0], kq(b)[1], qc[:, 0:C], qs[:, 0:C], True, True),
-               r=qk(t) + ["k%d" % b], w=["PB%d" % b])
-        op("s", lambda q: q.activation(Xt[:, PAD:XO], Xt[:, XO + 4 * C - PAD:XO + 4 * C], ACT.Copy),
-           r=xk(t), w=["X%dp" % t])
+            mm("PB", b, "k", 128 * b, xn, 0, C, qk(t) + ["k%d" % b])
+        act(Xt[:, PAD:XO], Xt[:, XO + 4 * C - PAD:XO + 4 * C], xk(t), ["X%dp" % t])
         for b in range(4):
-            op("s", lambda q: q.activation(T.H[:, PAD + b:PAD + 4 * C:4], bank(T.PB, b, 0, C), ACT.Copy, scale=0.25),
-               r=["PB%d" % b], w=["H%d" % b])
-            if t == 0 and b == 2:
-                op("s", lambda q: q.activation(T.S[:], T.hf[:, 1:449], ACT.Copy, scale=1.0 / 512), r=["hf"], w=["S"])
+            act(T.H[:, PAD + b:PAD + 4 * C:4], bank(T.PB, b, 0, C), ["PB%d" % b], ["H%d" % b], scale=0.25)
 
-        op("v", lambda q: q.tensor_copy(T.Pe[:], T.PA[:, 0:C:2]), r=["PA0"], w=["Pe"])
-        op("v", lambda q: q.tensor_tensor(T.dd[:, 1:C:2], T.PA[:, 1:C:2], T.Pe[:], A.subtract), r=["PA0", "Pe"], w=["d1"])
-        op("v", lambda q: q.tensor_tensor(T.dd[:, 2:C:2], T.Pe[:, 1:224], T.PA[:, 1:C - 2:2], A.subtract),
-           r=["PA0", "Pe"], w=["d0"])
-        op("v", lambda q: q.tensor_scalar(T.gg[:, 1:C], T.dd[:, 1:C], sgn, 0.0, A.mult, A.is_gt),
-           r=["d0", "d1", "sgn"], w=["gg"])
-        op("v", lambda q: q.tensor_tensor(T.fl[:, 1:C - 1], T.gg[:, 1:C - 1], T.gg[:, 2:C], A.is_gt), r=["gg"], w=["fl"])
-        op("v", lambda q: q.tensor_tensor_scan(T.Ln[:], T.fl[:], T.V[:, 1:C + 1], 0.0, A.max, A.min),
-           r=["fl", "V"], w=["Ln"])
-        op("v", lambda q: q.tensor_scalar(T.offE[:, 0:1], T.Ln[:, C - 1:C], 2048.0, cA, A.mult, A.add),
-           r=["Ln", "cA"], w=["offE"])
-        op("v", lambda q: q.tensor_copy(Xt[:, 0:PAD], Xt[:, PAD:XO + 4 * C].indirect(T.offE[:, 0:1])),
-           r=xk(t) + ["X%dp" % t, "offE"], w=["ET%d" % t])
-        op("v", lambda q: q.quantize_mx(qnc[:], qns[:], Xt[:, 0:512]), r=["ET%d" % t], w=["qn%d" % t])
-        wait("g", deps("g", ["qn%d" % t], []))
+        h, n = M // 2, C - M + 2
+        cp(T.Pe[:, 0:h], bank(T.PA, 0, 0, M, 2), ["PA0"], ["Pe0"])
+        tt(T.dd[:, 1:M:2], bank(T.PA, 0, 1, M, 2), T.Pe[:, 0:h], A.subtract, ["PA0", "Pe0"], ["d1_0"])
+        tt(T.dd[:, 2:M:2], T.Pe[:, 1:h], bank(T.PA, 0, 1, M - 2, 2), A.subtract, ["PA0", "Pe0"], ["d0_0"])
+        cp(T.Pe[:, h:C // 2], bank(T.PA, 1, 2, n, 2), ["PA1"], ["Pe1"])
+        ts(T.gg[:, 1:M], T.dd[:, 1:M], sgn, 0.0, A.mult, A.is_gt, ["d0_0", "d1_0", "sgn"], ["gg0"])
+        tt(T.dd[:, M + 1:C:2], bank(T.PA, 1, 3, n, 2), T.Pe[:, h:C // 2], A.subtract, ["PA1", "Pe1"], ["d1_1"])
+        tt(T.dd[:, M:C:2], T.Pe[:, h:C // 2], bank(T.PA, 1, 1, n - 2, 2), A.subtract, ["PA1", "Pe1"], ["d0_1"])
+        tt(T.fl[:, 1:h], T.gg[:, 1:h], T.gg[:, 2:h + 1], A.is_gt, ["gg0"], ["fl0"])
+        ts(T.gg[:, M:C], T.dd[:, M:C], sgn, 0.0, A.mult, A.is_gt, ["d0_1", "d1_1"], ["gg1"])
+        tt(T.fl[:, h:M - 1], T.gg[:, h:M - 1], T.gg[:, h + 1:M], A.is_gt, ["gg0"], ["fl1"])
+        tt(T.fl[:, M - 1:C - 1], T.gg[:, M - 1:C - 1], T.gg[:, M:C], A.is_gt, ["gg0", "gg1"], ["fl2"])
+        fk = ["fl0", "fl1", "fl2", "flp"]
+        hold(T.Ln[:], T.fl[:], T.V[:, 1:C + 1], fk + ["V0", "V1"], ["Ln"])
+        hold(T.Rk[:, 0:C - 1], T.fl[:, C - 1:0:-1], T.V[:, 0:C - 1], fk, ["Rk"])
+        ts(T.offE[:, 0:1], T.Ln[:, C - 1:C], 2048.0, cA, A.mult, A.add, ["Ln", "cA"], ["offE"])
+        hold(T.SA[:], T.M2[:, 0:224], T.Ln[:, 0:C:2], ["Ln", "M2"], ["SA"])
+        cp(Xt[:, 0:PAD], Xt[:, PAD:XO + 4 * C].indirect(T.offE[:, 0:1]), xk(t) + ["X%dp" % t, "offE"], ["ET%d" % t])
+        hold(T.SB[:], T.M2[:, 1:225], T.Rk[:, 0:C - 1:2], ["Rk", "M2"], ["SB"])
+        quant(nn, 0, 128, Xt[:, 0:512], ["ET%d" % t], [nn])
+        wait("g", deps("g", [nn], []))
         es = topo.engines(core, right)
         rid, pid = topo.addr(right)[:2]
         g.remote_dma_fused([
             RemoteDMATransfer(dst_ids=[DstId(rid=rid, pnc=pid)], dma_engine_mask=maskof(es[0::2]),
-                              remote_sem=T.sem["end%d" % t], src=qnc[:, 0:2].bitcast(U8), dst=qc[:, C:C + 2].bitcast(U8)),
+                              remote_sem=T.sem["end%d" % t], src=T[nn + "c"][:, 0:2].bitcast(U8),
+                              dst=T[xn + "c"][:, C:C + 2].bitcast(U8)),
             RemoteDMATransfer(dst_ids=[DstId(rid=rid, pnc=pid)], dma_engine_mask=maskof(es[1::2]),
-                              remote_sem=T.sem["end%d" % t], src=qns[:, 0:8], dst=qs[:, C:C + 8]),
+                              remote_sem=T.sem["end%d" % t], src=T[nn + "s"][:, 0:8], dst=T[xn + "s"][:, C:C + 8]),
         ], local_sem=T.sem.sent)
         count["sent"] += len(es)
         nend = len(topo.engines(left, core))
         count["end%d" % t] = nend
-
-        op("v", lambda q: q.tensor_tensor_scan(T.SA[:], T.M2[:, 0:224], T.Ln[:, 0:C:2], 0.0, A.max, A.min),
-           r=["Ln", "M2"], w=["SA"])
-        op("v", lambda q: q.tensor_tensor_scan(T.Rk[:, 0:C - 1], T.fl[:, C - 1:0:-1], T.V[:, 0:C - 1], 0.0, A.max, A.min),
-           r=["fl", "V"], w=["Rk"])
-        op("v", lambda q: q.tensor_scalar(T.offA[:], T.SA[:, 1:224:2], 2048.0, cA, A.mult, A.add),
-           r=["SA", "cA"], w=["offA"])
+        ts(T.offA[:], T.SA[:, 1:224:2], 2048.0, cA, A.mult, A.add, ["SA", "cA"], ["offA"])
 
         hk = ["H%d" % b for b in range(4)] + ["Hp"]
         for k in range(len(S1) - 1):
             a, z = S1[k], S1[k + 1]
-            op("s", lambda q: q.activation(T.T1[:, 16 * a:16 * z], T.H[:].indirect(T.offA[:, a:z]), ACT.Copy),
-               r=hk + ["offA"], w=["T1_%d" % k])
+            act(T.T1[:, 16 * a:16 * z], T.H[:].indirect(T.offA[:, a:z]), hk + ["offA"], ["T1_%d" % k])
 
-        op("v", lambda q: q.tensor_tensor_scan(T.SB[:], T.M2[:, 1:225], T.Rk[:, 0:C - 1:2], 0.0, A.max, A.min),
-           r=["Rk", "M2"], w=["SB"])
-        op("v", lambda q: q.tensor_tensor_scan(T.L2[:, 1:C + 1], T.fl[:], T.S[:], 0.0, A.max, A.min),
-           r=["fl", "S"], w=["L2"])
-        op("v", lambda q: q.tensor_scalar(T.offB[:], T.SB[:, 223:0:-2], -2048.0, cB, A.mult, A.add),
-           r=["SB", "cB"], w=["offB"])
-        op("v", lambda q: q.tensor_tensor_scan(T.SS[:], T.M4[:], T.L2[:], 0.0, A.max, A.min),
-           r=["L2", "L2a", "L2b", "M4"], w=["SS"])
-        op("v", lambda q: q.tensor_tensor_scan(T.SV[:], T.M4[:, 0:C], T.L2[:, 1:C + 1], 0.0, A.max, A.min),
-           r=["L2", "M4"], w=["SV"])
-        op("v", lambda q: q.tensor_scalar(T.offS[:, 0:113], T.SS[:, 3:452:4], 4096.0, c8, A.mult, A.add),
-           r=["SS", "cf"], w=["offS"])
-        op("v", lambda q: q.tensor_scalar(T.offV[:], T.SV[:, 3:C:4], 4096.0, c8, A.mult, A.add),
-           r=["SV", "cf"], w=["offV"])
+        hold(T.L2[:, 1:C + 1], T.fl[:], T.S[:], fk + ["S0", "S1"], ["L2"])
+        ts(T.offB[:], T.SB[:, 223:0:-2], -2048.0, cB, A.mult, A.add, ["SB", "cB"], ["offB"])
+        hold(T.SS[:], T.M4[:], T.L2[:], ["L2", "L2a", "L2b", "M4"], ["SS"])
+        hold(T.SV[:], T.M4[:, 0:C], T.L2[:, 1:C + 1], ["L2", "M4"], ["SV"])
+        ts(T.offS[:, 0:113], T.SS[:, 3:452:4], 4096.0, c8, A.mult, A.add, ["SS", "cf"], ["offS"])
+        ts(T.offV[:], T.SV[:, 3:C:4], 4096.0, c8, A.mult, A.add, ["SV", "cf"], ["offV"])
 
         fx = ["ABf%d" % e for e in range(8)]
         for k in range(len(S1) - 1):
             a, z = S1[k], S1[k + 1]
-            op("v", lambda q: q.tensor_tensor(T.AB[:, 16 * a:16 * z], T.H[:].indirect(T.offB[:, a:z]),
-                                              T.T1[:, 16 * a:16 * z], A.add),
-               r=hk + ["offB", "T1_%d" % k], w=["AB%d" % k] + (fx if k == 0 else []))
+            tt(T.AB[:, 16 * a:16 * z], T.H[:].indirect(T.offB[:, a:z]), T.T1[:, 16 * a:16 * z], A.add,
+               hk + ["offB", "T1_%d" % k], ["AB%d" % k] + (fx if k == 0 else []))
 
         if last:
-            op("s", lambda q: q.activation(T.omA[:], T.fl[:], ACT.Identity, bias=oms, scale=sgn),
-               r=["fl", "oms", "sgn"], w=["omA"])
+            act(T.omA[:], T.fl[:], fk + ["oms", "sgn"], ["omA"], ACT.Identity, bias=oms, scale=sgn)
             dma("y", T.om[:], T.omA[0:128:16, :], r=["omA"], w=["om"])
 
         for b in range(4):
-            op("t", lambda q: q.matmul_mx(bank(T.PA, b, 0, 128), kq(b)[0], kq(b)[1], qc[:, C - 126:C + 2],
-                                          qs[:, C - 126:C + 2], True, True),
-               r=qk(t) + ["k%d" % b], w=["PA%d" % b], extra=[("end%d" % t, nend, "r")])
+            mm("PA", b, "k", 128 * b, xn, C - 126, C + 2, qk(t) + ["k%d" % b], [("end%d" % t, nend, "r")])
         for b in range(4):
             for s in range(2):
                 e = 4 * s + b
-                op("s", lambda q: q.activation(T.AB[:, e:e + 1], bank(T.PA, b, 126 + s, 127 + s), ACT.Identity,
-                                               bias=T.AB[:, e:e + 1], scale=0.25),
-                   r=["PA%d" % b, "AB0"], w=["ABf%d" % e])
+                act(T.AB[:, e:e + 1], bank(T.PA, b, 126 + s, 127 + s), ["PA%d" % b, "AB0"], ["ABf%d" % e], ACT.Identity,
+                    bias=T.AB[:, e:e + 1], scale=0.25)
 
         ns = len(SUB) - 1
-        sb = [0] + [SUB[k] // 4 + 2 for k in range(1, ns)] + [113]
 
         def win(n1):
             upto = 1
@@ -325,82 +277,86 @@ def rank_program(g, core, T, topo):
                 upto += 1
             return T.AB[:, 0:16 * S1[upto]], ["AB%d" % k for k in range(upto)] + fx
 
-        for k in range(ns):
+        sb = [0, 30, 58, 88, 113]
+        for k in range(len(sb) - 1):
             a, z = sb[k], sb[k + 1]
             wv, keys = win(4 * z - 2)
-            op("s", lambda q: q.activation(T.T2[:, 16 * a:16 * z], wv.indirect(T.offS[:, a:z]), ACT.Copy),
-               r=keys + ["offS"], w=["T2_%d" % k])
+            act(T.T2[:, 16 * a:16 * z], wv.indirect(T.offS[:, a:z]), keys + ["offS"], ["T2_%d" % k])
         es = topo.engines(core, partner)
         rid, pid = topo.addr(partner)[:2]
         narr = 2 * len(topo.engines(partner, core))
+
+        def send(j):
+            c0, c1 = CH[j]
+            quant(en, c0, c1, T.E[:, 4 * c0:4 * c1], ["E%d" % i for i in range(ns) if SUB[i] < c1], ["qe%d_%d" % (t, j)])
+            wait("g", deps("g", ["qe%d_%d" % (t, j)], []))
+            sem = "arr%d_%d" % (t, j)
+            g.remote_dma(T[ln + "c"][:, c0:c1].bitcast(U8), T[en + "c"][:, c0:c1].bitcast(U8), T.sem[sem],
+                         T.sem.sent, pid, rid, maskof(es))
+            g.remote_dma(T[ln + "s"][:, c0:c1], T[en + "s"][:, c0:c1], T.sem[sem], T.sem.sent, pid, rid, maskof(es))
+            count["sent"] += 2 * len(es)
+            count[sem] = narr
+
+        def rest(b, parts):
+            for (c0, c1, key) in parts:
+                tt(T.G[:, C * b + c0:C * b + c1], bank(T.PB, b, c0, c1), T.E[:, 4 * c0 + b:4 * c1:4], A.subtract,
+                   ["E%d" % i for i in range(ns) if SUB[i] < c1] + ["PB%d" % b], [key])
+
         for k in range(ns):
             a, z = SUB[k], SUB[k + 1]
             wv, keys = win(z - 1)
-            op("v", lambda q: q.tensor_tensor(T.E[:, 4 * a:4 * z], wv.indirect(T.offV[:, a // 4:z // 4]),
-                                              T.T2[:, 4 * a + 4:4 * z + 4], A.add),
-               r=keys + ["offV"] + ["T2_%d" % j for j in range(k + 1)], w=["E%d" % k])
-            for j, (c0, c1) in enumerate(CH):
-                if c1 != z:
-                    continue
-                op("v", lambda q: q.quantize_mx(qec[:, c0:c1], qes[:, c0:c1], T.E[:, 4 * c0:4 * c1]),
-                   r=["E%d" % i for i in range(k + 1)], w=["qe%d_%d" % (t, j)])
-                wait("g", deps("g", ["qe%d_%d" % (t, j)], []))
-                sem = "arr%d_%d" % (t, j)
-                g.remote_dma(lec[:, c0:c1].bitcast(U8), qec[:, c0:c1].bitcast(U8), T.sem[sem], T.sem.sent, pid, rid,
-                             maskof(es))
-                g.remote_dma(les[:, c0:c1], qes[:, c0:c1], T.sem[sem], T.sem.sent, pid, rid, maskof(es))
-                count["sent"] += 2 * len(es)
-                count[sem] = narr
-
-        ek = ["E%d" % i for i in range(ns)]
-        for b in range(4):
-            op("v", lambda q: q.tensor_tensor(T.G[:, C * b:C * b + C], bank(T.PB, b, 0, C), T.E[:, b:4 * C:4], A.subtract),
-               r=ek + ["PB%d" % b], w=["G%d" % b])
-            op("s", lambda q: q.activation(T.G32[:, C * b:C * b + C], T.G[:, C * b:C * b + C], ACT.Copy, scale=32.0),
-               r=["G%d" % b], w=["G32_%d" % b])
+            tt(T.E[:, 4 * a:4 * z], wv.indirect(T.offV[:, a // 4:z // 4]), T.T2[:, 4 * a + 4:4 * z + 4], A.add,
+               keys + ["offV"] + ["T2_%d" % j for j in range(len(sb) - 1) if 4 * sb[j] <= z], ["E%d" % k])
+            if a == M:
+                send(0)
+        rest(0, [(0, M, "G0a")])
+        send(1)
+        for b in [1, 2, 3, 0]:
+            rest(b, [(M, C, "G0")] if b == 0 else [(0, C, "G%d" % b)])
+            act(T.G32[:, C * b:C * b + C], T.G[:, C * b:C * b + C], ["G%d" % b, "G0a"], ["G32_%d" % b], scale=32.0)
         if t == 0:
-            op("v", lambda q: q.quantize_mx(T.qvc[:], T.qvs[:], T.vb[:]), r=["vb"], w=["qv"])
+            quant("qv", 0, 128, T.vb[:], ["vb"], ["qv"])
         if last:
             dma("g", T.om[:], T.omA[4:128:16, :], r=["omA"], w=["om"], accum_op=A.add)
 
-        for j, (c0, c1) in enumerate(CH):
-            P, pn = (T.PA, "PA") if j % 2 == 0 else (T.PB, "PB")
-            n = c1 - c0
-            for b in range(4):
-                op("t", lambda q: q.matmul_mx(bank(P, b, 0, n), T.wqc[:, 128 * b:128 * b + 128],
-                                              T.wqs[:, 128 * b:128 * b + 128], lec[:, c0:c1], les[:, c0:c1], True, True),
-                   r=["wqc", "wqs"], w=["%s%d" % (pn, b)], extra=[("arr%d_%d" % (t, j), narr, "r")])
-            for b in range(4):
-                o = C * b
-                op("v", lambda q: q.tensor_tensor(T.X32[:, o + c0:o + c1], bank(P, b, 0, n), T.G32[:, o + c0:o + c1], A.add),
-                   r=["%s%d" % (pn, b), "G32_%d" % b], w=["X32_%d_%d" % (j, b)])
-                dst = Xn[:, XO + 4 * c0 + b:XO + 4 * c1:4]
-                kw = dict(r=["X32_%d_%d" % (j, b)], w=["X%d_%d_%d" % (t + 1, j, b)])
-                if b < 3:
-                    op("s", lambda q: q.activation(dst, T.X32[:, o + c0:o + c1], ACT.Copy, scale=0.03125), **kw)
-                else:
-                    op("v", lambda q: q.tensor_scalar(dst, T.X32[:, o + c0:o + c1], 0.03125, None, A.mult), **kw)
-            op("v", lambda q: q.quantize_mx(qcn[:, c0:c1], qsn[:, c0:c1], Xn[:, XO + 4 * c0:XO + 4 * c1]),
-               r=["X%d_%d_%d" % (t + 1, j, b) for b in range(4)], w=["qx%d_%d" % (t + 1, j)])
-            if last and j < nch - 1:
-                dma("y", T.oc[:, 4 * c0:4 * c1], qcn[:, c0:c1].bitcast(U8), r=["qx%d_%d" % (t + 1, j)])
+        def requant(j):
+            c0, c1 = CH[j]
+            quant("x%d" % (t + 1), c0, c1, Xn[:, XO + 4 * c0:XO + 4 * c1],
+                  ["X%d_%d_%d" % (t + 1, j, b) for b in range(4)], ["qx%d_%d" % (t + 1, j)])
 
-    qcn, qsn = T["qxc%d" % R], T["qxs%d" % R]
+        for j, (c0, c1) in enumerate(CH):
+            pn = "PA" if j % 2 == 0 else "PB"
+            order = [1, 2, 3, 0]
+            for b in order:
+                mm(pn, b, "wq", 128 * b, ln, c0, c1, ["wqc", "wqs"], [("arr%d_%d" % (t, j), narr, "r")])
+            for i, b in enumerate(order):
+                o = C * b
+                k32, kx = "X32_%d_%d" % (j, b), "X%d_%d_%d" % (t + 1, j, b)
+                tt(T.X32[:, o + c0:o + c1], bank(T[pn], b, 0, c1 - c0), T.G32[:, o + c0:o + c1], A.add,
+                   ["%s%d" % (pn, b), "G32_%d" % b], [k32])
+                dst = Xn[:, XO + 4 * c0 + b:XO + 4 * c1:4]
+                if i < 3 or j == 0:
+                    act(dst, T.X32[:, o + c0:o + c1], [k32], [kx], scale=0.03125)
+                else:
+                    if not last:
+                        requant(0)
+                    ts(dst, T.X32[:, o + c0:o + c1], 0.03125, None, A.mult, None, [k32], [kx])
+                if last and j == 1 and i == 1:
+                    requant(0)
+                    dma("y", T.oc[:, 0:4 * M], T.x2c[:, 0:M].bitcast(U8), r=["qx%d_0" % (t + 1)])
+        requant(1)
+
     for j, (c0, c1) in enumerate(CH):
-        n = c1 - c0
-        key = "qx%d_%d" % (R, j)
-        fin = j == nch - 1
-        yb = "PA%d" % j
-        op("t", lambda q: q.matmul_mx(bank(T.PA, j, 0, n), T.qvc[:], T.qvs[:], qcn[:, c0:c1], qsn[:, c0:c1], True, True),
-           r=[key, "qv"], w=[yb])
-        if not fin:
-            op("s", lambda q: q.activation(T.ysb[:, c0:c1], bank(T.PA, j, 0, n), ACT.Copy), r=[yb], w=["ysb%d" % j])
+        key, yb = "qx%d_%d" % (R, j), "PA%d" % j
+        mm("PA", j, "qv", 0, "x2", c0, c1, [key, "qv"])
+        if j < nch - 1:
+            act(T.ysb[:, c0:c1], bank(T.PA, j, 0, c1 - c0), [yb], ["ysb%d" % j])
             dma("y", T.y[:, c0:c1], T.ysb[:, c0:c1], r=["ysb%d" % j])
         else:
-            dma("y", T.oc[:, 4 * c0:4 * c1], qcn[:, c0:c1].bitcast(U8), r=[key])
+            dma("y", T.oc[:, 4 * c0:4 * c1], T.x2c[:, c0:c1].bitcast(U8), r=[key])
             for k in range(4):
-                dma("s" if k < 2 else "y", T.osc[4 * k:4 * k + 4, :], qsn[32 * k:32 * k + 4, 0:C], r=qk(R))
-            op("v", lambda q: q.tensor_copy(T.ysb[:, c0:c1], bank(T.PA, j, 0, n)), r=[yb], w=["ysb%d" % j])
+                dma("ssyy"[k], T.osc[4 * k:4 * k + 4, :], T.x2s[32 * k:32 * k + 4, 0:C], r=qk(R))
+            cp(T.ysb[:, c0:c1], bank(T.PA, j, 0, c1 - c0), [yb], ["ysb%d" % j])
             dma("s", T.y[:, c0:c1], T.ysb[:, c0:c1], r=["ysb%d" % j])
 
     wait("g", [(sem, count[sem], "x") for sem in count if count[sem] > 0])

from concourse.bass import DstId, RemoteDMATransfer
from concourse.mybir import dt, AluOpType, ActivationFunctionType

C = 448
R = 2
STEP = [2, 1]
PAD = 16
XO = 2 * PAD
CH = [(0, 224), (224, 448)]
SUB = [0, 112, 224, 248, 344, 448]
S1 = [0, 58, 112]
CODE = "float8_e4m3fn_x4"

SCRATCH = {"PA": ("psum", [128, 2048], "float32"), "PB": ("psum", [128, 2048], "float32")}
for _d, _l in {
    "bfloat16": [("X0", XO + 4 * C), ("X1", XO + 4 * C), ("X2", XO + 4 * C), ("ub", 512), ("vb", 512), ("kt", 516),
                 ("kf", 516), ("hf", 226), ("r4", 452), ("S", C), ("M4", 452), ("M2", 226), ("dd", C), ("gg", C),
                 ("fl", C), ("L2", 452), ("SV", C), ("SS", 452), ("H", PAD + 4 * C), ("T1", 4 * C), ("AB", 4 * C),
                 ("T2", 4 * C + 16), ("E", 4 * C), ("G", 4 * C), ("G32", 4 * C), ("X32", 4 * C)],
    "float16": [("V", 450), ("Ln", C), ("Rk", C), ("SA", 224), ("SB", 224)],
    "float32": [("cf", 8), ("cd", 8), ("Pe", 224), ("omA", C), ("ysb", C)],
    "int32": [("pi", 2), ("ci", 8), ("uoi", 8)],
    "uint16": [("uoff", 8), ("offE", 2), ("offA", 112), ("offB", 112), ("offV", 112), ("offS", 114)],
}.items():
    for _n, _w in _l:
        SCRATCH[_n] = ("sbuf", [128, _w], _d)
for _n, _w in [("qu", 128), ("qr", 128), ("qv", 128), ("wq", 512), ("k", 512), ("x0", C + 16), ("x1", C + 16),
               ("x2", C + 16), ("n0", 128), ("n1", 128), ("e0", C), ("e1", C), ("l0", C), ("l1", C)]:
    SCRATCH[_n + "c"] = ("sbuf", [128, _w], CODE)
    SCRATCH[_n + "s"] = ("sbuf", [128, _w], "uint8")

SEMAPHORES = ["cv", "cs", "ct", "cg", "sent"]
SEMAPHORES += ["d%d" % _i for _i in range(24)]
SEMAPHORES += ["end%d" % _t for _t in range(R)]
SEMAPHORES += ["arr%d_%d" % (_t, _k) for _t in range(R) for _k in range(len(CH))]

A = AluOpType
ACT = ActivationFunctionType
U8 = dt.uint8
U32 = dt.uint32


def rank_program(g, core, T, topo):
    rank = T.rank_of(core)
    if rank is None:
        return
    N = len(T.cores)
    Q = {"v": g.vector, "s": g.scalar, "t": g.tensor, "g": g, "y": g.sync}
    CNT = {"v": "cv", "s": "cs", "t": "ct", "g": "cg"}
    count = {"cv": 0, "cs": 0, "ct": 0, "cg": 0, "sent": 0}
    waited = {e: {} for e in Q}
    writer, readers = {}, {}
    ndma = [0]

    def wait(e, toks):
        need = {}
        for (sem, val, src) in toks:
            if val > waited[e].get(sem, 0) and val > need.get(sem, 0):
                need[sem] = val
        for sem in need:
            Q[e].wait_ge(T.sem[sem], need[sem])
            waited[e][sem] = need[sem]

    def deps(e, r, w):
        toks = []
        for k in r:
            if k in writer:
                toks.append(writer[k])
            if k[:2] in ("PA", "PB"):
                toks += [x for x in readers.get(k, []) if x[2] != e]
        for k in w:
            if k in writer:
                toks.append(writer[k])
            toks += readers.get(k, [])
        return toks

    def done(tok, r, w):
        for k in r:
            readers.setdefault(k, []).append(tok)
        for k in w:
            writer[k] = tok
            readers[k] = []

    def op(e, fn, r=(), w=(), extra=()):
        wait(e, deps(e, r, w) + list(extra))
        sem = CNT[e]
        fn(Q[e]).then_inc(T.sem[sem], 1)
        count[sem] += 1
        done((sem, count[sem], e), r, w)

    def dma(e, out, in_, r=(), w=(), extra=(), **kw):
        wait(e, deps(e, r, w) + list(extra))
        sem = "d%d" % ndma[0]
        ndma[0] += 1
        Q[e].dma_start(out, in_, **kw).then_inc(T.sem[sem], 16)
        count[sem] = 16
        tok = (sem, 16, "dma")
        done(tok, r, w)
        return tok

    def maskof(es):
        m = 0
        for x in es:
            m |= 1 << x
        return m

    def ts(out, in0, s1, s2, o0, o1, r, w):
        if s2 is None:
            op("v", lambda q: q.tensor_scalar(out, in0, s1, None, o0), r, w)
        else:
            op("v", lambda q: q.tensor_scalar(out, in0, s1, s2, o0, o1), r, w)

    def tt(out, in0, in1, o, r, w):
        op("v", lambda q: q.tensor_tensor(out, in0, in1, o), r, w)

    def cp(out, in_, r, w):
        op("v", lambda q: q.tensor_copy(out, in_), r, w)

    def hold(out, pick, val, r, w):
        op("v", lambda q: q.tensor_tensor_scan(out, pick, val, 0.0, A.max, A.min), r, w)

    def act(out, in_, r, w, func=ACT.Copy, **kw):
        op("s", lambda q: q.activation(out, in_, func, **kw), r, w)

    def quant(name, a, z, in_, r, w):
        op("v", lambda q: q.quantize_mx(T[name + "c"][:, a:z], T[name + "s"][:, a:z], in_), r, w)

    def bank(P, b, a, z, step=1):
        return P[:, 512 * b + a:512 * b + z:step]

    def mm(P, b, wn, wa, xn, a, z, r, extra=()):
        op("t", lambda q: q.matmul_mx(T[P][:, 512 * b:512 * b + z - a], T[wn + "c"][:, wa:wa + 128],
                                      T[wn + "s"][:, wa:wa + 128], T[xn + "c"][:, a:z], T[xn + "s"][:, a:z], True, True),
           r, ["%s%d" % (P, b)], extra)

    right = T.cores[(rank + 1) % N]
    left = T.cores[(rank - 1) % N]
    X = [T.X0, T.X1, T.X2]
    nch = len(CH)
    M = CH[0][1]

    tx = dma("y", T.X0[:, XO:XO + 4 * C], T.x[:], w=["X0_0", "X0_1"])
    dma("s", T.ub[:], T.u[:], w=["ub"])
    dma("y", T.wqc[:].bitcast(U8), T.wc[:], w=["wqc"], extra=[tx])
    dma("y", T.wqs[:], T.ws[:], w=["wqs"])
    dma("y", T.vb[:], T.v[:], w=["vb"])

    fi = dict(allow_small_or_imprecise_dtypes=True)
    op("g", lambda q: q.iota(T.pi[:, 0:1], [[0, 1]], 0, 1), w=["pi"])
    op("g", lambda q: q.iota(T.uoi[:], [[16, 8]], 0, 0), w=["uoi"])
    op("g", lambda q: q.iota(T.kf[:], [[1, 516]], 0, -4, **fi), w=["kf"])
    op("g", lambda q: q.iota(T.hf[:], [[1, 226]], 0, 0, **fi), w=["hf"])
    op("g", lambda q: q.iota(T.r4[:], [[0, 113], [1, 4]], 0, 0, **fi), w=["r4"])

    op("v", lambda q: q.memset(T.fl[:, 0:C:C - 1], 0.0), w=["flp"])
    op("v", lambda q: q.memset(T.H[:, 0:PAD], 0.0), w=["Hp"])
    for j, (sh, m) in enumerate([(0, 3), (2, 3), (2, 1), (2, 2), (0, 7)]):
        ts(T.ci[:, j:j + 1], T.pi[:, 0:1], sh, m, A.logical_shift_right, A.bitwise_and, ["pi"], ["ci%d" % j])
    cp(T.uoff[:], T.uoi[:], ["uoi"], ["uoff"])
    op("v", lambda q: q.memset(T.L2[:, 0:1], 0.0), w=["L2a"])
    op("v", lambda q: q.memset(T.L2[:, 449:452], 223.0 / 512), w=["L2b"])
    cp(T.cf[:, 0:5], T.ci[:, 0:5], ["ci%d" % j for j in range(5)], ["cf"])
    ct, cq, cs, ch2, c8 = [T.cf[:, j:j + 1] for j in range(5)]
    sgn, cA, cB, oms = [T.cd[:, j:j + 1] for j in range(4)]
    act(sgn, cs, ["cf"], ["sgn"], ACT.Identity, bias=1.0, scale=-2.0)
    act(cA, ct, ["cf"], ["cA"], ACT.Identity, bias=float(PAD - 4))
    act(cB, ct, ["cf"], ["cB"], ACT.Identity, bias=float(PAD + 4 * (C - 1)))
    act(oms, cs, ["cf"], ["oms"], ACT.Identity, bias=1.0, scale=-1.0)
    ts(T.kt[:], T.kf[:], 3.0, None, A.is_equal, None, ["kf"], ["kt"])
    for b in range(4):
        quant("k", 128 * b, 128 * b + 128, T.kt[:, 3 - b:515 - b], ["kt"], ["k%d" % b])
    quant("qu", 0, 128, T.ub[:], ["ub"], ["qu"])
    ts(T.V[:, 0:450:2], T.hf[:, 0:225], 1.0 / 256, None, A.mult, None, ["hf"], ["V0"])
    ts(T.V[:, 1:450:2], T.hf[:, 0:225], 1.0 / 256, 1.0 / 512, A.mult, A.add, ["hf"], ["V1"])
    cp(T.qrc[:].bitcast(U32), T.quc[:].bitcast(U32).indirect(T.uoff[:]), ["qu", "uoff"], ["qrc"])
    act(T.qrs[:], T.qus[:].indirect(T.uoff[:]), ["qu", "uoff"], ["qrs"])
    act(T.S[:, 0:C:2], T.hf[:, 0:224], ["hf"], ["S0"], scale=1.0 / 512)
    act(T.S[:, 1:C:2], T.hf[:, 1:225], ["hf"], ["S1"], scale=1.0 / 512)

    def xk(t):
        if t == 0:
            return ["X0_%d" % k for k in range(nch)]
        return ["X%d_%d_%d" % (t, k, b) for k in range(nch) for b in range(4)]

    def qk(t):
        return ["qx%d_%d" % (t, k) for k in range(nch)]

    quant("x0", 0, M, T.X0[:, XO:XO + 4 * M], ["X0_0"], ["qx0_0"])
    quant("x0", M, C, T.X0[:, XO + 4 * M:XO + 4 * C], ["X0_1"], ["qx0_1"])
    ts(T.M2[:, 0:225], T.r4[:, 0:450:2], ch2, None, A.is_equal, None, ["r4", "cf"], ["M2"])
    ts(T.M4[:], T.r4[:], cq, None, A.is_equal, None, ["r4", "cf"], ["M4"])

    for t in range(R):
        last = t == R - 1
        partner = T.cores[rank ^ STEP[t]]
        Xt, Xn = X[t], X[t + 1]
        xn, nn, en, ln = "x%d" % t, "n%d" % t, "e%d" % t, "l%d" % t

        mm("PA", 0, "qr", 0, xn, 0, M, ["qx%d_0" % t, "qrc", "qrs"])
        mm("PA", 1, "qr", 0, xn, M - 2, C, qk(t) + ["qrc", "qrs"])
        for b in range(4):
            mm("PB", b, "k", 128 * b, xn, 0, C, qk(t) + ["k%d" % b])
        act(Xt[:, PAD:XO], Xt[:, XO + 4 * C - PAD:XO + 4 * C], xk(t), ["X%dp" % t])
        for b in range(4):
            act(T.H[:, PAD + b:PAD + 4 * C:4], bank(T.PB, b, 0, C), ["PB%d" % b], ["H%d" % b], scale=0.25)

        h, n = M // 2, C - M + 2
        cp(T.Pe[:, 0:h], bank(T.PA, 0, 0, M, 2), ["PA0"], ["Pe0"])
        tt(T.dd[:, 1:M:2], bank(T.PA, 0, 1, M, 2), T.Pe[:, 0:h], A.subtract, ["PA0", "Pe0"], ["d1_0"])
        tt(T.dd[:, 2:M:2], T.Pe[:, 1:h], bank(T.PA, 0, 1, M - 2, 2), A.subtract, ["PA0", "Pe0"], ["d0_0"])
        cp(T.Pe[:, h:C // 2], bank(T.PA, 1, 2, n, 2), ["PA1"], ["Pe1"])
        ts(T.gg[:, 1:M], T.dd[:, 1:M], sgn, 0.0, A.mult, A.is_gt, ["d0_0", "d1_0", "sgn"], ["gg0"])
        tt(T.dd[:, M + 1:C:2], bank(T.PA, 1, 3, n, 2), T.Pe[:, h:C // 2], A.subtract, ["PA1", "Pe1"], ["d1_1"])
        tt(T.dd[:, M:C:2], T.Pe[:, h:C // 2], bank(T.PA, 1, 1, n - 2, 2), A.subtract, ["PA1", "Pe1"], ["d0_1"])
        tt(T.fl[:, 1:h], T.gg[:, 1:h], T.gg[:, 2:h + 1], A.is_gt, ["gg0"], ["fl0"])
        ts(T.gg[:, M:C], T.dd[:, M:C], sgn, 0.0, A.mult, A.is_gt, ["d0_1", "d1_1"], ["gg1"])
        tt(T.fl[:, h:M - 1], T.gg[:, h:M - 1], T.gg[:, h + 1:M], A.is_gt, ["gg0"], ["fl1"])
        tt(T.fl[:, M - 1:C - 1], T.gg[:, M - 1:C - 1], T.gg[:, M:C], A.is_gt, ["gg0", "gg1"], ["fl2"])
        fk = ["fl0", "fl1", "fl2", "flp"]
        hold(T.Ln[:], T.fl[:], T.V[:, 1:C + 1], fk + ["V0", "V1"], ["Ln"])
        hold(T.Rk[:, 0:C - 1], T.fl[:, C - 1:0:-1], T.V[:, 0:C - 1], fk, ["Rk"])
        ts(T.offE[:, 0:1], T.Ln[:, C - 1:C], 2048.0, cA, A.mult, A.add, ["Ln", "cA"], ["offE"])
        hold(T.SA[:], T.M2[:, 0:224], T.Ln[:, 0:C:2], ["Ln", "M2"], ["SA"])
        cp(Xt[:, 0:PAD], Xt[:, PAD:XO + 4 * C].indirect(T.offE[:, 0:1]), xk(t) + ["X%dp" % t, "offE"], ["ET%d" % t])
        hold(T.SB[:], T.M2[:, 1:225], T.Rk[:, 0:C - 1:2], ["Rk", "M2"], ["SB"])
        quant(nn, 0, 128, Xt[:, 0:512], ["ET%d" % t], [nn])
        wait("g", deps("g", [nn], []))
        es = topo.engines(core, right)
        rid, pid = topo.addr(right)[:2]
        g.remote_dma_fused([
            RemoteDMATransfer(dst_ids=[DstId(rid=rid, pnc=pid)], dma_engine_mask=maskof(es[0::2]),
                              remote_sem=T.sem["end%d" % t], src=T[nn + "c"][:, 0:2].bitcast(U8),
                              dst=T[xn + "c"][:, C:C + 2].bitcast(U8)),
            RemoteDMATransfer(dst_ids=[DstId(rid=rid, pnc=pid)], dma_engine_mask=maskof(es[1::2]),
                              remote_sem=T.sem["end%d" % t], src=T[nn + "s"][:, 0:8], dst=T[xn + "s"][:, C:C + 8]),
        ], local_sem=T.sem.sent)
        count["sent"] += len(es)
        nend = len(topo.engines(left, core))
        count["end%d" % t] = nend
        ts(T.offA[:], T.SA[:, 1:224:2], 2048.0, cA, A.mult, A.add, ["SA", "cA"], ["offA"])

        hk = ["H%d" % b for b in range(4)] + ["Hp"]
        for k in range(len(S1) - 1):
            a, z = S1[k], S1[k + 1]
            act(T.T1[:, 16 * a:16 * z], T.H[:].indirect(T.offA[:, a:z]), hk + ["offA"], ["T1_%d" % k])

        hold(T.L2[:, 1:C + 1], T.fl[:], T.S[:], fk + ["S0", "S1"], ["L2"])
        ts(T.offB[:], T.SB[:, 223:0:-2], -2048.0, cB, A.mult, A.add, ["SB", "cB"], ["offB"])
        hold(T.SS[:], T.M4[:], T.L2[:], ["L2", "L2a", "L2b", "M4"], ["SS"])
        hold(T.SV[:], T.M4[:, 0:C], T.L2[:, 1:C + 1], ["L2", "M4"], ["SV"])
        ts(T.offS[:, 0:113], T.SS[:, 3:452:4], 4096.0, c8, A.mult, A.add, ["SS", "cf"], ["offS"])
        ts(T.offV[:], T.SV[:, 3:C:4], 4096.0, c8, A.mult, A.add, ["SV", "cf"], ["offV"])

        fx = ["ABf%d" % e for e in range(8)]
        for k in range(len(S1) - 1):
            a, z = S1[k], S1[k + 1]
            tt(T.AB[:, 16 * a:16 * z], T.H[:].indirect(T.offB[:, a:z]), T.T1[:, 16 * a:16 * z], A.add,
               hk + ["offB", "T1_%d" % k], ["AB%d" % k] + (fx if k == 0 else []))

        if last:
            act(T.omA[:], T.fl[:], fk + ["oms", "sgn"], ["omA"], ACT.Identity, bias=oms, scale=sgn)
            dma("y", T.om[:], T.omA[0:128:16, :], r=["omA"], w=["om"])

        for b in range(4):
            mm("PA", b, "k", 128 * b, xn, C - 126, C + 2, qk(t) + ["k%d" % b], [("end%d" % t, nend, "r")])
        for b in range(4):
            for s in range(2):
                e = 4 * s + b
                act(T.AB[:, e:e + 1], bank(T.PA, b, 126 + s, 127 + s), ["PA%d" % b, "AB0"], ["ABf%d" % e], ACT.Identity,
                    bias=T.AB[:, e:e + 1], scale=0.25)

        ns = len(SUB) - 1

        def win(n1):
            upto = 1
            while 2 * S1[upto] - 1 < min((n1 + 1) // 2, 223):
                upto += 1
            return T.AB[:, 0:16 * S1[upto]], ["AB%d" % k for k in range(upto)] + fx

        sb = [0, 30, 58, 88, 113]
        for k in range(len(sb) - 1):
            a, z = sb[k], sb[k + 1]
            wv, keys = win(4 * z - 2)
            act(T.T2[:, 16 * a:16 * z], wv.indirect(T.offS[:, a:z]), keys + ["offS"], ["T2_%d" % k])
        es = topo.engines(core, partner)
        rid, pid = topo.addr(partner)[:2]
        narr = 2 * len(topo.engines(partner, core))

        def send(j):
            c0, c1 = CH[j]
            quant(en, c0, c1, T.E[:, 4 * c0:4 * c1], ["E%d" % i for i in range(ns) if SUB[i] < c1], ["qe%d_%d" % (t, j)])
            wait("g", deps("g", ["qe%d_%d" % (t, j)], []))
            sem = "arr%d_%d" % (t, j)
            g.remote_dma(T[ln + "c"][:, c0:c1].bitcast(U8), T[en + "c"][:, c0:c1].bitcast(U8), T.sem[sem],
                         T.sem.sent, pid, rid, maskof(es))
            g.remote_dma(T[ln + "s"][:, c0:c1], T[en + "s"][:, c0:c1], T.sem[sem], T.sem.sent, pid, rid, maskof(es))
            count["sent"] += 2 * len(es)
            count[sem] = narr

        def rest(b, parts):
            for (c0, c1, key) in parts:
                tt(T.G[:, C * b + c0:C * b + c1], bank(T.PB, b, c0, c1), T.E[:, 4 * c0 + b:4 * c1:4], A.subtract,
                   ["E%d" % i for i in range(ns) if SUB[i] < c1] + ["PB%d" % b], [key])

        for k in range(ns):
            a, z = SUB[k], SUB[k + 1]
            wv, keys = win(z - 1)
            tt(T.E[:, 4 * a:4 * z], wv.indirect(T.offV[:, a // 4:z // 4]), T.T2[:, 4 * a + 4:4 * z + 4], A.add,
               keys + ["offV"] + ["T2_%d" % j for j in range(len(sb) - 1) if 4 * sb[j] <= z], ["E%d" % k])
            if a == M:
                send(0)
        rest(0, [(0, M, "G0a")])
        send(1)
        for b in [1, 2, 3, 0]:
            rest(b, [(M, C, "G0")] if b == 0 else [(0, C, "G%d" % b)])
            act(T.G32[:, C * b:C * b + C], T.G[:, C * b:C * b + C], ["G%d" % b, "G0a"], ["G32_%d" % b], scale=32.0)
        if t == 0:
            quant("qv", 0, 128, T.vb[:], ["vb"], ["qv"])
        if last:
            dma("g", T.om[:], T.omA[4:128:16, :], r=["omA"], w=["om"], accum_op=A.add)

        def requant(j):
            c0, c1 = CH[j]
            quant("x%d" % (t + 1), c0, c1, Xn[:, XO + 4 * c0:XO + 4 * c1],
                  ["X%d_%d_%d" % (t + 1, j, b) for b in range(4)], ["qx%d_%d" % (t + 1, j)])

        for j, (c0, c1) in enumerate(CH):
            pn = "PA" if j % 2 == 0 else "PB"
            order = [1, 2, 3, 0]
            for b in order:
                mm(pn, b, "wq", 128 * b, ln, c0, c1, ["wqc", "wqs"], [("arr%d_%d" % (t, j), narr, "r")])
            for i, b in enumerate(order):
                o = C * b
                k32, kx = "X32_%d_%d" % (j, b), "X%d_%d_%d" % (t + 1, j, b)
                tt(T.X32[:, o + c0:o + c1], bank(T[pn], b, 0, c1 - c0), T.G32[:, o + c0:o + c1], A.add,
                   ["%s%d" % (pn, b), "G32_%d" % b], [k32])
                dst = Xn[:, XO + 4 * c0 + b:XO + 4 * c1:4]
                if i < 3 or j == 0:
                    act(dst, T.X32[:, o + c0:o + c1], [k32], [kx], scale=0.03125)
                else:
                    if not last:
                        requant(0)
                    ts(dst, T.X32[:, o + c0:o + c1], 0.03125, None, A.mult, None, [k32], [kx])
                if last and j == 1 and i == 1:
                    requant(0)
                    dma("y", T.oc[:, 0:4 * M], T.x2c[:, 0:M].bitcast(U8), r=["qx%d_0" % (t + 1)])
        requant(1)

    for j, (c0, c1) in enumerate(CH):
        key, yb = "qx%d_%d" % (R, j), "PA%d" % j
        mm("PA", j, "qv", 0, "x2", c0, c1, [key, "qv"])
        if j < nch - 1:
            act(T.ysb[:, c0:c1], bank(T.PA, j, 0, c1 - c0), [yb], ["ysb%d" % j])
            dma("y", T.y[:, c0:c1], T.ysb[:, c0:c1], r=["ysb%d" % j])
        else:
            dma("y", T.oc[:, 4 * c0:4 * c1], T.x2c[:, c0:c1].bitcast(U8), r=[key])
            for k in range(4):
                dma("ssyy"[k], T.osc[4 * k:4 * k + 4, :], T.x2s[32 * k:32 * k + 4, 0:C], r=qk(R))
            cp(T.ysb[:, c0:c1], bank(T.PA, j, 0, c1 - c0), [yb], ["ysb%d" % j])
            dma("s", T.y[:, c0:c1], T.ysb[:, c0:c1], r=["ysb%d" % j])

    wait("g", [(sem, count[sem], "x") for sem in count if count[sem] > 0])
